import numpy as np, ml_dtypes
CORES = [51,54,179,182]
N = 4
BF = ml_dtypes.bfloat16
def gentries(a):
    return np.ascontiguousarray(a.reshape(8, 16, -1).transpose(0, 2, 1)).reshape(8, -1)
def gtable(e):
    e = np.asarray(e); return np.ascontiguousarray(e.reshape(8, -1, 16).transpose(0, 2, 1)).reshape(128, -1).astype(np.int32)
C, D, S, CAP, TH, HOP = 1536, 256, 4, 32, 12, 1
R = C // 16
def inverse(A):
    O = np.zeros_like(A); np.put_along_axis(O, A, np.broadcast_to(np.arange(C), A.shape), -1)
    return O
def estates(A, Y):
    V = np.zeros_like(Y)
    for k in range(16): V += np.take_along_axis(Y, A[:, :, k:k + 1, :], 3)
    return V
def judge(A, O, V, Y, h, z):
    n = h.shape[1]
    ca = np.take_along_axis(A, h[:, None, :], 2)
    yv = np.take_along_axis(Y, ca.reshape(8, 1, 16 * n), 2).reshape(8, 16, 16, n)
    k = np.argmax(np.add.reduce(np.minimum(yv, z[:, :, None, :]), axis=1), axis=1)
    a = np.take_along_axis(ca, k[:, None, :], 1)[:, 0]
    co = np.take_along_axis(O, a[:, None, :], 2)
    vv = np.take_along_axis(V, co.reshape(8, 1, 16 * n), 2).reshape(8, 16, 16, n)
    vc = np.take_along_axis(V, h[:, None, :], 2)
    over = np.add.reduce((vv > vc[:, :, None, :]).astype(np.int64), axis=1)
    j = np.argmax(over, axis=1)[:, None, :]
    return k, a, np.take_along_axis(co, j, 1)[:, 0], np.take_along_axis(over, j, 1)[:, 0]
def meets(x):
    eq = np.any(x[:, None, :, None] == x[None, :, None, :], axis=(2, 3))
    return np.any(np.tril(eq, -1), axis=1)
def exchange(A, O, V, Y, c, f, k, a):
    b = A[k, f]
    ok = ~(meets(np.stack([c, f], 1)) | meets(np.stack([a, b], 1)))
    c, f, k, a, b = c[ok], f[ok], k[ok], a[ok], b[ok]
    A[k, c] = b; A[k, f] = a; O[k, a] = f; O[k, b] = c
    dv = Y[:, b] - Y[:, a]
    V[:, c] += dv; V[:, f] -= dv
def cities(rng):
    rc = np.argsort(rng.random((N, 8, C)), axis=-1); ra = np.argsort(rng.random((N, 8, C)), axis=-1)
    key = rng.random((N, 8, 16, C)); key[:, :, 1:, :R] -= 1.0
    A = np.take_along_axis(ra[:, :, None, :], np.argsort(key, axis=-1), 3)
    A = np.take_along_axis(A, np.argsort(rc, axis=-1)[:, :, None, :], 3)
    m = np.zeros((N, 8, C), bool); np.put_along_axis(m, ra[:, :, :R], True, -1)
    Y = rng.integers(0, 16, (N, 8, 16, C)); Y = np.where(m[:, :, None, :], (Y >> 1) + 8, Y)
    return A, Y, np.ascontiguousarray(rc[:, :, :R])
def duties(rng, rc, n):
    h = np.where(rng.random((N, 8, n)) < 0.125, np.take_along_axis(rc, rng.integers(0, R, (N, 8, n)), 2), rng.integers(0, C, (N, 8, n)))
    top = rng.choice(np.array([0, 1, 3, 7, 7, 11, 15, 15, 15, 15]), (N, 8, 1, n))
    return h, rng.integers(0, top + 1, (N, 8, 16, n))
def ring(rng, A, Y, g, T):
    pc = np.argsort(rng.random((N, C)), axis=-1); pa = np.argsort(rng.random((N, C)), axis=-1)
    for q in range(N):
        A[q, g][:, pc[q]] = pa[q][(np.arange(C)[None, :] + np.arange(16)[:, None]) % C]
        Y[q, g][:, pa[q]] = T[q][:, np.arange(C) % 16]
    return pc
def pack(A, Y, h, z):
    O = inverse(A); V = estates(A, Y)
    w = lambda x: np.ascontiguousarray(x.reshape(N, 128, -1)).astype(np.float32).astype(BF)
    return {"ao": np.ascontiguousarray((A + 4096 * O).reshape(N, 128, C)).astype(np.int32), "yd": w(Y), "ve": w(V), "hd": np.stack([gtable(x) for x in h]), "zc": w(z)}
def setup_inputs(rng):
    A, Y, rc = cities(rng); h, z = duties(rng, rc, D)
    return pack(A, Y, h, z)
def setup_inputs_room(rng):
    A, Y, rc = cities(rng); h4, z4 = duties(rng, rc, 4 * D); O = inverse(A); V = estates(A, Y)
    h = np.zeros((N, 8, D), np.int64); z = np.zeros((N, 8, 16, D), np.int64)
    for q in range(N):
        k, a, f, m = judge(A[q], O[q], V[q], Y[q], h4[q], z4[q]); prop = (m < TH) & (f != h4[q])
        for g in range(8):
            yes = np.nonzero(prop[g])[0]; no = np.nonzero(~prop[g])[0]; ver = np.nonzero(m[g] >= TH)[0]
            if len(yes) == 0: yes = no
            if len(no) == 0: no = yes
            n = int(rng.choice(np.array([0, 1, CAP - 1, CAP, CAP + 1, D])))
            if q == 0: n = (CAP, CAP + 1, D, CAP - 1, 1, 0, CAP, CAP + 1)[g]
            if n == 0 and q % 2 == 0 and len(ver) > 0: no = ver
            ix = rng.permutation(np.concatenate([np.resize(rng.permutation(yes), n), np.resize(rng.permutation(no), D - n)]))
            h[q, g] = h4[q, g, ix]; z[q, g] = z4[q, g][:, ix]
    return pack(A, Y, h, z)
def setup_inputs_clash(rng):
    A, Y, rc = cities(rng); h, z = duties(rng, rc, D); iq = np.arange(N)
    T = rng.integers(0, 11, (N, 16, 16)); w = rng.integers(0, 16, N); T[iq, :, w] = 15
    p2 = ring(rng, A, Y, 2, T)
    T = rng.integers(0, 11, (N, 16, 16)); c4 = rng.integers(0, C, N); ks = np.argsort(rng.random((N, 15)), axis=-1)[:, :2] + 1
    T[iq, :8, (c4 + ks[:, 0]) % 16] = 15; T[iq, 8:, (c4 + ks[:, 1]) % 16] = 15
    p4 = ring(rng, A, Y, 4, T)
    e = int(rng.integers(0, C)); s = int(rng.integers(0, C)); r16 = np.arange(16)
    for q in range(N):
        at = np.argmax(A[q, 6] == s, axis=1); A[q, 6][r16, at] = A[q, 6][r16, e]; A[q, 6][r16, e] = s
    O = inverse(A)
    few = rng.integers(0, C, (N, 8, 24)); hf = np.take_along_axis(few, rng.integers(0, 24, (N, 8, D)), 2)
    st = np.argsort(rng.random((N, 8, C)), axis=-1)[:, :, None, :12]
    own = np.take_along_axis(O, st, 3).reshape(N, 8, 192); ho = np.take_along_axis(own, rng.integers(0, 192, (N, 8, D)), 2)
    Y2 = Y.copy(); np.put_along_axis(Y2, np.broadcast_to(st, (N, 8, 16, 12)), 15, 3)
    Y[:, 1::2] = Y2[:, 1::2]; h[:, ::2] = hf[:, ::2]; h[:, 1::2] = ho[:, 1::2]
    z[:, 1::2] = rng.integers(8, 16, (N, 4, 16, D))
    gap = C // CAP // 16 * 16
    for q in range(N):
        d = rng.permutation(D)[:CAP]; k = rng.integers(1, 16, CAP)
        z[q, 2] = 0; z[q, 2][:, d] = 15; h[q, 2, d] = p2[q, gap * np.arange(CAP) + (w[q] - k) % 16]
    kind = (np.arange(D)[None, :] + rng.integers(0, 2, (N, 1))) % 2
    h[:, 4] = p4[iq, c4][:, None]; z[:, 4] = np.where((np.arange(16) < 8)[None, :, None] == (kind == 0)[:, None, :], 15, 0)
    h[int(rng.integers(0, N)), 6] = e
    return pack(A, Y, h, z)
def setup_inputs_ties(rng):
    A, Y, rc = cities(rng); h, z = duties(rng, rc, D)
    lo = rng.integers(0, 4, (N, 8, 1, 1)); hi = lo + rng.integers(1, 12, (N, 8, 1, 1))
    Y = np.where(rng.random((N, 8, 16, C)) < 0.5, lo, hi)
    z = np.where(rng.random((N, 8, 1, D)) < 0.5, rng.integers(0, 16, (N, 8, 1, D)), z)
    g = rng.permutation(8); Y[:, g[0]] = rng.integers(1, 16, (N, 1, 1)); z[:, g[1]] = 0
    Y[:, g[2]] = rng.integers(14, 16, (N, 16, C)); z[:, g[2]] = np.where(rng.random((N, 1, D)) < 0.5, 15, rng.integers(14, 16, (N, 16, D)))
    return pack(A, Y, h, z)
def setup_inputs_ends(rng):
    A, Y, rc = cities(rng); h, z = duties(rng, rc, D)
    A[:, 1] = np.arange(C); A[:, 2] = (np.arange(C)[None, :] + np.arange(16)[:, None]) % C; A[:, 3] = A[:, 2]
    Y[..., 0] = 15; Y[..., C - 1] = 15; O = inverse(A)
    T = rng.integers(0, 16, (N, 16, 16)); Y[:, 3] = T[:, :, np.arange(C) % 16]
    own = np.ascontiguousarray(O[..., [0, C - 1]]).reshape(N, 8, 32)
    u = rng.random((N, 8, D)); e = rng.choice(np.array([0, C - 1]), (N, 8, D))
    h = np.where(u < 0.4, np.take_along_axis(own, rng.integers(0, 32, (N, 8, D)), 2), np.where(u < 0.5, e, h))
    h[..., 0] = 0; h[..., D - 1] = C - 1
    return pack(A, Y, h, z)
def setup_inputs_spread(rng):
    A, Y, rc = cities(rng); h, z = duties(rng, rc, D)
    s = np.exp2(4 * rng.random((N, 8, 1, C))) * np.exp2(-2 * rng.random((N, 8, 16, 1)))
    Y = np.minimum((s * rng.random((N, 8, 16, C))).astype(np.int64), 15)
    Y[rng.random(Y.shape) < 0.05] = 15
    z = np.minimum((np.exp2(5 * rng.random((N, 8, 1, D))) * rng.random((N, 8, 16, D))).astype(np.int64), 15)
    return pack(A, Y, h, z)
def check_inputs(d):
    bad = []
    for k, hi in (("yd", 15), ("zc", 15), ("ve", 240)):
        x = np.asarray(d[k]).astype(np.float32)
        if not np.all((x >= 0) & (x <= hi) & (x == np.floor(x))): bad.append("range of " + k)
    if np.min(d["hd"]) < 0 or np.max(d["hd"]) > C - 1: bad.append("range of hd")
    ao = np.asarray(d["ao"]).astype(np.int64).reshape(N, 8, 16, C); A = ao & 4095; O = ao >> 12
    if np.min(ao) < 0 or np.max(A) > C - 1 or np.max(O) > C - 1: return bad + ["range of ao"]
    m = np.zeros(A.shape, bool); np.put_along_axis(m, A, True, -1)
    if not np.all(m): bad.append("a row of A is no permutation")
    if not np.all(np.take_along_axis(O, A, 3) == np.arange(C)): bad.append("O is not the inverse of A")
    if not bad:
        Y = np.asarray(d["yd"]).astype(np.float32).astype(np.int64).reshape(N, 8, 16, C)
        if not np.all(estates(A, Y) == np.asarray(d["ve"]).astype(np.float32).astype(np.int64).reshape(N, 8, 16, C)): bad.append("ve is not the sum of the yields")
    return bad
def reference(ao, yd, ve, hd, zc):
    w = ao.astype(np.int64).reshape(N, 8, 16, C); A = w & 4095; O = w >> 12
    Y = yd.astype(np.float32).astype(np.int64).reshape(N, 8, 16, C); V = ve.astype(np.float32).astype(np.int64).reshape(N, 8, 16, C)
    z = zc.astype(np.float32).astype(np.int64).reshape(N, 8, 16, D); h = np.stack([gentries(x) for x in hd]).astype(np.int64)
    log = []
    for t in range(S):
        new = []
        for q in range(N):
            k, a, f, m = judge(A[q], O[q], V[q], Y[q], h[q], z[q])
            for g in range(8):
                ix = np.nonzero((m[g] < TH) & (f[g] != h[q, g]))[0][:CAP]
                exchange(A[q, g], O[q, g], V[q, g], Y[q, g], h[q, g, ix], f[g, ix], k[g, ix], a[g, ix])
            new.append(np.where(m >= TH, f, h[q]))
        h = np.stack(new); log.append(h)
        if t < S - 1:
            h = np.roll(h, HOP, axis=0); z = np.roll(z, HOP, axis=0)
    return {"vo": V.reshape(N, 128, C).astype(np.float32).astype(BF), "ho": np.stack(log, axis=2).reshape(N, 8, S * D).astype(np.float32)}

@@ -1,0 +1,573 @@
+from concourse.mybir import AluOpType, AxisListType, ActivationFunctionType
+
+ALU = AluOpType
+ACT = ActivationFunctionType
+C, D, S, N = 1536, 256, 4, 4
+CH = 32
+PATH = ("ssvvvvvs", "ssvvvvhs")
+VRUNS = ((64, 128, "g"), (128, 192, "g"))
+CUT = ((), ())
+POST = ((0, 8), (8, 16))
+VSUB = 32
+BOOST = {'vV1': 3000, 'vV2': 3000, 'sVC1': 4000, 'sVCT1': 4000, 'gJX1': 1500, 'vCA1': -1000, 'vCO2': -4000,
+         'vSC2': -200, 'gVQ7': 200, 'sG6': 500, 'vMK1': 4000, 'gPI1': 500, 'vPC1': -4000, 'vKKI1': -3500}
+PLAN = {}
+MAG = 12582912.0
+BIG = 8192.0
+GC, SCT, CYC, PEC = 1.56, 3.8, 1.0, 0.5
+LX, LQ = 100.0, 60.0
+
+F, B, I, U, H = "float32", "bfloat16", "int32", "uint16", "float16"
+SB = {
+    "AO": (C, I), "AI": (C, I), "A": (C + 64, F), "O": (C + 64, F), "Y": (C, B), "V": (C + 64, B), "IOTA": (C, F),
+    "M0": (4096, B), "M1": (4096, B), "G0": (4096, B), "G1": (4096, B), "REP": (2048, B), "ONES": (512, B),
+    "Z0": (D, B), "VR": (4096, B), "VQ": (1024, B), "VCT": (D, B), "VC": (D, B),
+    "H16": (16, U), "CA16": (D, U), "CO16": (D, U), "CAF": (D + 16, F), "COF": (D + 16, F), "AF": (D + 16, F),
+    "FR": (D + 16, F), "OH": (D + 16, F), "SC0": (128, F), "SC1": (128, F), "XM0": (128, F), "XM1": (128, F),
+    "K1I": (16, I), "K2I": (16, I), "AIL": (16, I), "KKI": (16, I), "FI": (16, I), "A16": (16, U), "K16": (16, U),
+    "F16": (16, U), "NV": (16, F), "DF": (16, F), "E1": (16, F), "P16": (16, U), "NH16": (16, U),
+    "PR": (D, B), "R": (D, B), "JK": (D, B), "JV": (D, B), "CN": (2, F), "D16": (2, U), "TH2": (2, F),
+    "OHS": (32, F), "X": (128, H), "BA": (64, F), "DA": (32, F), "BW": (64, F), "DO": (32, F),
+    "BV": (64, B), "DV": (64, B), "YAB": (64, B), "LSC": (128, F), "L": (8, F), "L16": (8, U), "E": (8, F),
+    "DF0": (256, F), "DF1": (256, F), "MN": (2, F), "OK": (2, F), "OFF": (8, U),
+    "PI": (2, I), "PJ": (2, I), "PC": (8, F), "JN": (128, F), "JX": (128, F), "JG": (128, F), "JS": (128, F),
+    "IDB": (128, B), "NID": (128, B), "IDF": (128, F), "MASK": (128, F), "BLK": (128, H), "UD": (8, F), "WP": (8, B),
+    "WN": (8, B), "WH": (8, B), "KROW": (128, B), "NEG": (128, F), "CT": (128, F), "CT2": (128, F), "MK0": (128, B),
+    "MK1": (128, B), "OFS": (8, F), "DUM": (8, F), "CLI": (8, I), "CL": (8, U), "OHT": (16, F), "THR": (16, F),
+    "J8": (8, F), "J4": (8, F), "CB": (2, F),
+}
+for _t in range(S):
+    SB["HI%d" % _t] = (16, I)
+    SB["NH%d" % _t] = (16, I)
+    SB["ZR%d" % _t] = (4096 + D, B)
+    SB["HR%d" % _t] = (D, F)
+SCRATCH = {k: ("sbuf", [128, v[0]], v[1]) for k, v in SB.items()}
+for _b in range(8):
+    SCRATCH["P%d" % _b] = ("psum", [128, 512], F)
+SEMAPHORES = (["qv", "qs", "qt", "qg", "sent"] + ["d%d" % i for i in range(16)]
+              + ["za%d" % i for i in range(1, S)] + ["ha%d" % i for i in range(1, S)])
+
+
+def bits(lo, hi, st):
+    if st == 1:
+        return ((1 << (hi - lo)) - 1) << lo
+    m = 0
+    for c in range(lo, hi, st):
+        m |= 1 << c
+    return m
+
+
+def build(T, ops):
+    tags = {}
+
+    def a(name, lo=0, hi=None, st=1, p0=0, p1=128):
+        if hi is None:
+            hi = SCRATCH[name][1][1]
+        ap = T[name][p0:p1, lo:hi:st] if st != 1 else T[name][p0:p1, lo:hi]
+        m = bits(lo, hi, st)
+        if SCRATCH[name][0] == "psum":
+            m = sum(m << (512 * k) for k in range(p0 // 32, (p1 + 31) // 32))
+        return (ap, name, m, len(range(lo, hi, st)))
+
+    def ind(win, off):
+        return (win[0].indirect(off[0]), win[1], win[2], 16 * off[3], off)
+
+    def two(*xs):
+        return all(SCRATCH[x[1]][2] in (B, H, U) for x in xs)
+
+    def add(q, fn, outs, ins, cost, **kw):
+        rd, wr = [], []
+        for x in ins:
+            if isinstance(x, tuple):
+                rd.append((x[1], x[2]))
+                if len(x) == 5:
+                    rd.append((x[4][1], x[4][2]))
+        for x in outs:
+            wr.append((x[1], x[2]))
+            if len(x) == 5:
+                rd.append((x[4][1], x[4][2]))
+        o = dict(q=q, fn=fn, rd=rd, wr=wr, cost=cost, lat=0.0, kind="c")
+        nm = q + (outs[0][1] if outs else "").rstrip("0123456789")
+        tags[nm] = tags.get(nm, 0) + 1
+        o["tag"] = nm + str(tags[nm])
+        o.update(kw)
+        ops.append(o)
+        return len(ops) - 1
+
+    def v(x):
+        return x[0] if isinstance(x, tuple) else x
+
+    def vc(out, in0, per):
+        if len(out) == 5:
+            return 50 + out[3] * SCT * CYC
+        if len(in0) == 5:
+            return 50 + in0[3] * GC * CYC
+        return 40 + max(64, out[3] * per) * CYC
+
+    def cp(out, in_):
+        add("v", lambda e, k: e.tensor_copy(out[0], in_[0]), [out], [in_], vc(out, in_, 0.5 if two(out, in_) else 1))
+
+    def tt(out, in0, in1, op):
+        per = 1 if SCRATCH[in0[1]][0] == "psum" else 2
+        add("v", lambda e, k: e.tensor_tensor(out[0], in0[0], in1[0], op), [out], [in0, in1], vc(out, in0, per))
+
+    def ts(out, in0, s1, op0, s2=None, op1=None):
+        if op1 is None:
+            fn = lambda e, k: e.tensor_scalar(out[0], in0[0], v(s1), None, op0)
+        else:
+            fn = lambda e, k: e.tensor_scalar(out[0], in0[0], v(s1), v(s2), op0, op1)
+        add("v", fn, [out], [in0, s1, s2], vc(out, in0, 0.5 if two(out, in0) else 1))
+
+    def scan(out, d0, d1, init, op0, op1):
+        add("v", lambda e, k: e.tensor_tensor_scan(out[0], d0[0], d1[0], v(init), op0, op1), [out], [d0, d1, init],
+            vc(out, d0, 0.5 if two(out, d0, d1) else 1))
+
+    def red(out, in_, op, ab=False):
+        if ab:
+            fn = lambda e, k: e.tensor_reduce(out[0], in_[0], AxisListType.X, op, apply_absolute_value=True)
+        else:
+            fn = lambda e, k: e.tensor_reduce(out[0], in_[0], AxisListType.X, op)
+        add("v", fn, [out], [in_], 40 + max(64, in_[3]) * CYC)
+
+    def mset(out, c):
+        add("v", lambda e, k: e.memset(out[0], c), [out], [], 40 + max(64, out[3] * (0.5 if two(out) else 1)) * CYC)
+
+    def act(out, in_, func=ACT.Identity, bias=None, scale=1.0, acc=None):
+        kw = {}
+        if bias is not None:
+            kw["bias"] = v(bias)
+        if scale != 1.0:
+            kw["scale"] = scale
+        if acc is not None:
+            kw["accum_out"] = acc[0]
+        cost = 65 + in_[3] * GC * CYC if len(in_) == 5 else 80 + max(64, in_[3]) * CYC
+        add("s", lambda e, k: e.activation(out[0], in_[0], func, **kw), [out] + ([acc] if acc else []), [in_, bias], cost)
+
+    def mm(out, lt, rh, grp):
+        c = max(min(64, lt[3]), rh[3]) * (4 if SCRATCH[lt[1]][2] == F else 1) * PEC + 10
+        add("t", lambda e, k: e.matmul(out[0], lt[0], rh[0], k[0], k[1]), [out], [lt, rh], c, grp=grp, lat=60.0)
+
+    def iota(out, pat, base, cm):
+        if SCRATCH[out[1]][2] == I:
+            fn = lambda e, k: e.iota(out[0], pat, base, cm)
+        else:
+            fn = lambda e, k: e.iota(out[0], pat, base, cm, allow_small_or_imprecise_dtypes=True)
+        add("g", fn, [out], [], 130 + 2 * out[3] * CYC)
+
+    def copy_on(q, out, in_):
+        if q == "g":
+            add("g", lambda e, k: e.affine_select(out[0], in_[0], [[0, out[3]]], ALU.is_ge, 0.0, 0, 0), [out], [in_],
+                170 + 2 * out[3] * CYC)
+        elif q == "s":
+            act(out, in_, ACT.Copy)
+        else:
+            cp(out, in_)
+
+    def dma(q, out, in_, outs, ins, lat, after=()):
+        return add(q, lambda e, k: e.dma_start(out, in_), outs, ins, 60.0, kind="d", lat=lat, after=list(after))
+
+    def remote(src, dst, hop, sem, lat, after=()):
+        j = add("g", None, [], [src], 300.0, kind="r", src=src[0], dst=dst[0], hop=hop, sem=sem, after=list(after))
+        add("x", None, [dst], [], 0.0, kind="x", lat=lat, after=[j], hop=hop, sem=sem)
+        return j
+
+    vch = [c for c in range(8) if PATH[0][c] == "v"] or [0]
+    z0, z1 = CH * vch[0], CH * (vch[-1] + 1)
+    zt = 16 * (z1 - z0)
+
+    def segs(s, h):
+        r = []
+        for c in range(4 * h, 4 * h + 4):
+            k = PATH[s][c] in "sw"
+            if r and r[-1][2] == k and r[-1][0] % 64 == 0 and c not in CUT[s]:
+                r[-1][1] += CH
+            else:
+                r.append([c * CH, (c + 1) * CH, k])
+        return r
+
+    def turned(dst, lo, src, s, gid):
+        for h in (0, 1):
+            if s == 0 or PATH[s][4 * h:4 * h + 4] != "vvvv":
+                mm(a("P7", 128 * h, 128 * h + 128), a(src, 128 * h, 128 * h + 128), a("IDB"), (gid, h))
+                act(a(dst, lo + 128 * h, lo + 128 * h + 128), a("P7", 128 * h, 128 * h + 128), ACT.Copy)
+
+    hc = C // 2
+    j = dma("s", T.Z0[:], T.zc[:], [a("Z0")], [], 2300.0)
+    dma("s", T.HI0[:], T.hd[:], [a("HI0")], [], 2300.0, [j])
+    j = dma("y", T.AO[:, 0:hc], T.ao[:, 0:hc], [a("AO", 0, hc)], [], 4000.0)
+    j = dma("y", T.AO[:, hc:C], T.ao[:, hc:C], [a("AO", hc, C)], [], 6000.0, [j])
+    j = dma("y", T.Y[:], T.yd[:], [a("Y")], [], 8000.0, [j])
+    dma("y", T.V[:, 0:C], T.ve[:], [a("V", 0, C)], [], 10000.0, [j])
+
+    iota(a("PI", 0, 1), [[0, 1]], 0, 1)
+    iota(a("JN"), [[1, 128]], 0, 0)
+    iota(a("JX"), [[0, 8], [1, 16]], 0, 0)
+    iota(a("JG"), [[1, 8], [0, 16]], 0, 0)
+    iota(a("JS"), [[0, 4], [1, 32]], 0, 0)
+    iota(a("CLI"), [[16, 8]], 15, 0)
+    iota(a("J8"), [[0, 4], [int(BIG), 2]], 0, 0)
+    iota(a("J4"), [[0, 4], [16, 2]], C, 0)
+    ts(a("PJ", 0, 1), a("PI", 0, 1), 15, ALU.bitwise_and)
+    ts(a("PJ", 1, 2), a("PI", 0, 1), 4, ALU.logical_shift_right)
+    pp, p16, pg, p17, ph, p32, q15, pf = (a("PC", j, j + 1) for j in range(8))
+    cp(pp, a("PI", 0, 1))
+    cp(a("PC", 1, 3), a("PJ"))
+    ts(p17, p16, 1.0, ALU.add)
+    ts(ph, p16, 0.5, ALU.add)
+    ts(p32, p16, 16.0, ALU.add)
+    ts(q15, p16, -1.0, ALU.mult, 15.0, ALU.add)
+    ts(pf, p16, 15.0, ALU.is_lt, 4096.0, ALU.mult)
+    mset(a("CB"), -511.0 / 512)
+    ts(a("IDB"), a("JN"), pp, ALU.is_equal)
+    ts(a("NID"), a("JN"), pp, ALU.is_equal, -1.0, ALU.mult)
+    ts(a("IDF"), a("JN"), pp, ALU.is_equal)
+    ts(a("MASK"), a("JX"), p16, ALU.is_equal)
+    ts(a("BLK"), a("JG"), pg, ALU.is_equal)
+    ts(a("UD"), a("JN", 0, 8), pg, ALU.is_equal)
+    for nm, w in (("WP", 32768.0), ("WN", -32768.0), ("WH", 16384.0)):
+        ts(a(nm), a("JN", 0, 8), pg, ALU.is_equal, w, ALU.mult)
+    ts(a("KROW"), a("JX"), -2048.0, ALU.mult, 30720.0, ALU.add)
+    ts(a("NEG"), a("JX"), 0.0, ALU.is_equal, -1.0e9, ALU.mult)
+    ts(a("CT"), a("JX"), p16, ALU.is_equal, -1.0e6, ALU.mult)
+    ts(a("CT2"), a("JX"), p17, ALU.is_equal, 4096.0, ALU.mult)
+    tt(a("CT"), a("CT"), a("CT2"), ALU.add)
+    ts(a("MK0"), a("JS"), p16, ALU.is_ge, BIG, ALU.mult)
+    ts(a("MK1"), a("JS"), p32, ALU.is_ge, BIG, ALU.mult)
+    ts(a("OFS"), a("J8"), pf, ALU.add)
+    ts(a("DUM"), a("J4"), p16, ALU.add)
+    cp(a("CL"), a("CLI"))
+    ts(a("OHT"), a("JN", 0, 16), q15, ALU.is_equal)
+    c0 = 0
+    for c in range(1, 9):
+        if c == 8 or (PATH[1][c] in "sw") != (PATH[1][c0] in "sw"):
+            mset(a("THR", 2 * c0, 2 * c), (4.0 if PATH[1][c0] in "sw" else 12.0) * 32768.0)
+            c0 = c
+    for nm in ("CAF", "COF", "AF", "FR", "OH"):
+        mset(a(nm, D, D + 16), 0.0)
+    for nm in ("A", "O", "V"):
+        mset(a(nm, C, C + 64), 0.0)
+    mset(a("ONES"), 1.0)
+    for j in range(4):
+        if any(PATH[s][c] != "v" for s in (0, 1) for c in (j, j + 4)):
+            o, i = a("REP", 512 * j, 512 * j + 512), a("ONES")
+            add("g", lambda e, k, o=o, i=i, j=j: e.affine_select(o[0], i[0], [[-1, CH], [0, 16]], ALU.is_equal, 0.0,
+                                                                 -CH * j, 1), [o], [i], 170 + 1024 * CYC)
+    for j in range(3):
+        iota(a("IOTA", 512 * j, 512 * j + 512), [[1, 512]], 512 * j, 0)
+
+    for lo in (0, hc):
+        ts(a("AI", lo, lo + hc), a("AO", lo, lo + hc), 4095, ALU.bitwise_and)
+        cp(a("A", lo, lo + hc), a("AI", lo, lo + hc))
+        ts(a("O", lo, lo + hc), a("AO", lo, lo + hc), 1.0 / 4096, ALU.mult, MAG, ALU.add)
+
+    for k in range(16):
+        act(a("ZR0", k, zt, 16), a("Z0", z0, z1), ACT.Copy)
+    turned("ZR0", zt, "Z0", 0, "z0")
+
+    def send_costs(t, after):
+        remote(a("ZR0", 0, zt + D), a("ZR%d" % t, 0, zt + D), t, "za%d" % t, 14000.0, after)
+
+    tabA, tabO, tabV, tabY = a("A", 0, C), a("O", 0, C), a("V", 0, C), a("Y")
+    nd = [0]
+
+    def stage(t, s, h):
+        M, G, offs, keyf = "M%d" % s, "G%d" % s, ("CA16", "CO16")[s], ("CAF", "COF")[s]
+        tab = (tabY, tabV)[s]
+        tr = a("VCT", 128 * h, 128 * h + 128) if s else a("ZR%d" % t, zt + 128 * h, zt + 128 * h + 128)
+        bank, gid = "P%d" % (2 * s + h), ("k", t, s, h)
+        mm(a(bank, 0, 128), a(keyf, 128 * h, 128 * h + 128), a("IDF"), gid)
+        for c in range(4 * h, 4 * h + 4):
+            d, kind = c * CH, PATH[s][c]
+            if kind != "v":
+                g_, db, m = a(G, 16 * d, 16 * d + 512), a("P%d" % (4 + nd[0] % 2)), a(M, 16 * d, 16 * d + 512)
+                nd[0] += 1
+                copy_on("v" if kind == "w" else "s", g_, ind(tab, a(offs, d, d + CH)))
+                mm(db, tr, a("REP", 512 * (c % 4), 512 * (c % 4) + 512), ("d", nd[0]))
+                if kind == "h":
+                    tt(m, db, g_, (ALU.min, ALU.is_lt)[s])
+                else:
+                    mm(db, a("NID"), g_, ("d", nd[0]))
+                    if s == 0:
+                        act(m, db, ACT.Relu)
+                    else:
+                        act(m, db, ACT.Sign, -0.5, -1.0)
+            else:
+                for d in range(d, d + CH, VSUB):
+                    rep = a("VR", 16 * d, 16 * (d + VSUB)) if s else a("ZR%d" % t, 16 * (d - z0), 16 * (d - z0 + VSUB))
+                    tt(a(M, 16 * d, 16 * (d + VSUB)), ind(tab, a(offs, d, d + VSUB)), rep, (ALU.min, ALU.is_gt)[s])
+        for d0, d1, sc in segs(s, h):
+            w = a(("WN", "WH")[s] if sc else "WP")
+            for k in range(16):
+                mm(a(bank, k, 128, 16, d0 - 128 * h, d1 - 128 * h), a(M, 16 * d0 + k, 16 * d1, 16), w, gid)
+        mm(a(bank, 0, 128), a("ONES", 0, 128, 1, 0, 1), a("KROW", 0, 128, 1, 0, 1), gid)
+        sc_, xm = a("SC%d" % h), a("XM%d" % h)
+        scan(sc_, a("NEG"), a(bank, 0, 128), 0.0, ALU.add, ALU.max)
+        tt(xm, ind(sc_, a("CL")), a("MASK"), ALU.mult)
+        lp = a("P6", 16 * s + 8 * h, 16 * s + 8 * h + 8)
+        mm(lp, xm, a("UD"), ("l", t, s, h))
+        cp(a(("K1I", "K2I")[s], 8 * h, 8 * h + 8), lp)
+
+    for t in range(S):
+        last = t == S - 1
+        tags.clear()
+        HI, NH = "HI%d" % t, "NH%d" % t
+        cp(a("H16"), a(HI))
+        for h in (0, 1):
+            cp(a("CA16", 128 * h, 128 * h + 128), ind(tabA, a("H16", 8 * h, 8 * h + 8)))
+        act(a("CAF", 0, D), ind(tabA, a("H16")), ACT.Copy)
+        act(a("VC"), ind(tabV, a("H16")), ACT.Copy)
+        turned("VCT", 0, "VC", 1, ("v", t))
+        for d0, d1, q in VRUNS:
+            for k in range(4):
+                copy_on(q, a("VQ", 4 * d0 + k, 4 * d1, 4), a("VC", d0, d1))
+            for k in range(4):
+                copy_on(q, a("VR", 16 * d0 + k, 16 * d1, 4), a("VQ", 4 * d0, 4 * d1))
+        if t == 0:
+            send_costs(1, [])
+        for h in (0, 1):
+            stage(t, 0, h)
+            l = (8 * h, 8 * h + 8)
+            r = (128 * h, 128 * h + 128)
+            ts(a("AIL", *l), a("K1I", *l), 2047, ALU.bitwise_and)
+            cp(a("A16", *l), a("AIL", *l))
+            ts(a("CO16", *r), ind(tabO, a("A16", *l)), -MAG, ALU.add)
+            act(a("COF", *r), ind(tabO, a("A16", *l)), ACT.Identity, -MAG)
+        ts(a("KKI"), a("K1I"), 11, ALU.arith_shift_right, 15, ALU.bitwise_and)
+        cp(a("K16"), a("KKI"))
+        act(a("OH", 0, D), ind(a("OHT"), a("K16")), ACT.Copy)
+        for h in (0, 1):
+            stage(t, 1, h)
+        for l in POST:
+            r = (16 * l[0], 16 * l[1])
+            ts(a("FI", *l), a("K2I", *l), 2047, ALU.bitwise_and)
+            tt(a("NV", *l), a("K2I", *l), a("THR", *l), ALU.is_lt)
+            cp(a("F16", *l), a("FI", *l))
+            tt(a("DF", *l), a("FI", *l), a(HI, *l), ALU.subtract)
+            tt(a("E1", *l), a("DF", *l), a("NV", *l), ALU.mult)
+            ts(a("P16", *l), a("E1", *l), 0.0, ALU.not_equal)
+            tt(a(NH, *l), a("FI", *l), a("E1", *l), ALU.subtract)
+            act(a("AF", *r), ind(tabA, a("F16", *l)), ACT.Copy)
+            act(a("FR", *r), ind(a("IOTA"), a("F16", *l)), ACT.Copy)
+            cp(a("PR", *r), ind(a("JN"), a("P16", *l)))
+            scan(a("R", *r), a("PR", *r), a("PR", *r), a("R", 127, 128) if l[0] else 0.0, ALU.add, ALU.max)
+        if not last:
+            j = remote(a(NH), a("HI%d" % (t + 1)), 1, "ha%d" % (t + 1), 2500.0)
+            if t + 2 < S:
+                send_costs(t + 2, [j])
+        cp(a("NH16"), a(NH))
+        act(a("HR%d" % t), ind(a("IOTA"), a("NH16")), ACT.Copy)
+        dma("y", T.ho[:, t * D:(t + 1) * D], T["HR%d" % t][0:128:16, :], [], [a("HR%d" % t)], 2000.0)
+        act(a("JK"), a("R"), ACT.Sign, ph, -1.0, a("CN", 0, 1))
+        ts(a("JV"), a("R"), p32, ALU.is_le)
+        red(a("CN", 1, 2), a("JV"), ALU.add)
+        ts(a("D16", 0, 1), a("CN", 0, 1), 0.5, ALU.mult, 128.0, ALU.add)
+        cp(a("D16", 1, 2), a("CN", 1, 2))
+        ts(a("TH2"), a("CN"), 255.5, ALU.is_ge, 1.0e9, ALU.mult)
+        d16 = a("D16")
+        cp(a("OHS"), ind(a("OH"), d16))
+        xs = [a("X", 32 * j, 32 * j + 32) for j in range(4)]
+        for j, nm in enumerate(("COF", "FR", "CAF", "AF")):
+            tt(xs[j], ind(a(nm), d16), a("OHS"), ALU.mult)
+        r0, r1 = a("P0", 0, 128), a("P1", 0, 128)
+        mm(r1, a("IDB"), a("MK1"), ("e", t, 1))
+        mm(r0, a("IDB"), a("MK0"), ("e", t, 0))
+        mm(r1, a("BLK"), a("X"), ("e", t, 1))
+        mm(r0, a("BLK"), a("X"), ("e", t, 0))
+        if not last:
+            act(a("BA", 0, 32), ind(a("CAF"), d16), ACT.Copy)
+            act(a("BA", 32, 64), ind(a("AF"), d16), ACT.Copy)
+            tt(a("DA"), xs[3], xs[2], ALU.subtract)
+            tt(a("DO"), xs[1], xs[0], ALU.subtract)
+        scan(a("LSC"), a("CT"), r1, 0.0, ALU.add, ALU.max)
+        tt(a("L"), a("LSC", 15, 128, 16), a("OFS"), ALU.subtract)
+        for j in range(4):
+            lo = 64 * (j // 2)
+            ts(a("DF0", 64 * j, 64 * j + 64), a("P0", lo, lo + 64), a("L", 2 * j, 2 * j + 1), ALU.not_equal)
+            act(a("DF1", 64 * j, 64 * j + 64), a("P1", lo, lo + 64), ACT.Identity, a("L", 2 * j + 1, 2 * j + 2), -1.0)
+        cp(a("L16"), a("L"))
+        tt(a("E"), a("L"), a("DUM"), ALU.subtract)
+        act(a("JK"), a("DF0"), ACT.Identity, a("CB", 0, 1), 1.0, a("MN", 0, 1))
+        red(a("MN", 1, 2), a("DF1"), ALU.min, True)
+        tt(a("OK"), a("MN"), a("TH2"), ALU.is_gt)
+        for j in range(2):
+            ts(a("OFF", j, 8, 2), a("E", j, 8, 2), a("OK", j, j + 1), ALU.mult, a("DUM", j, j + 1), ALU.add)
+        act(a("YAB"), ind(tabY, a("L16", 4, 8)), ACT.Copy)
+        act(a("BV"), ind(tabV, a("L16", 0, 4)), ACT.Copy)
+        tt(a("DV", 0, 32), a("YAB", 32, 64), a("YAB", 0, 32), ALU.subtract)
+        act(a("DV", 32, 64), a("DV", 0, 32), ACT.Identity, None, -1.0)
+        if not last:
+            act(a("BW"), ind(tabO, a("L16", 4, 8)), ACT.Copy)
+            for j, op in ((0, ALU.add), (1, ALU.subtract)):
+                tt(ind(a("A"), a("OFF", 2 * j, 2 * j + 2)), a("BA", 32 * j, 32 * j + 32), a("DA"), op)
+        for j in (0, 1):
+            tt(ind(a("V"), a("OFF", 2 * j, 2 * j + 2)), a("BV", 32 * j, 32 * j + 32), a("DV", 32 * j, 32 * j + 32), ALU.add)
+        if not last:
+            for j, op in ((0, ALU.add), (1, ALU.subtract)):
+                tt(ind(a("O"), a("OFF", 4 + 2 * j, 6 + 2 * j)), a("BW", 32 * j, 32 * j + 32), a("DO"), op)
+    dma("y", T.vo[:], T.V[:, 0:C], [], [tabV], 4000.0)
+
+
+def plan(ops):
+    n = len(ops)
+    seen = {}
+    deps = [set() for _ in range(n)]
+    for j, o in enumerate(ops):
+        for wr, lst in ((False, o["rd"]), (True, o["wr"])):
+            for name, m in lst:
+                psum = SCRATCH[name][0] == "psum"
+                for i, mi, wi in seen.get(name, ()):
+                    if ((wi or wr) and mi & m) or (psum and ops[i]["q"] != o["q"]):
+                        deps[j].add(i)
+        for wr, lst in ((False, o["rd"]), (True, o["wr"])):
+            for name, m in lst:
+                old = seen.get(name, [])
+                if wr:
+                    old = [x for x in old if x[1] & ~m]
+                seen[name] = old + [(j, m, wr)]
+        deps[j].discard(j)
+    behind = [set(o.get("after", ())) for o in ops]
+    succ = [[] for _ in range(n)]
+    for j in range(n):
+        for i in deps[j] | behind[j]:
+            succ[i].append(j)
+
+    def gap(i, j):
+        if (ops[i]["q"] == "t" and ops[j]["q"] == "t") or i not in deps[j]:
+            return 0.0
+        return ops[i]["lat"] + (LQ if ops[i]["q"] == ops[j]["q"] else LX)
+
+    prio = [0.0] * n
+    for i in range(n - 1, -1, -1):
+        prio[i] = ops[i]["cost"] + max([gap(i, j) + prio[j] for j in succ[i]] + [ops[i]["lat"]])
+    return place(ops, deps, behind, succ, gap, prio, BOOST), deps
+
+
+def place(ops, deps, behind, succ, gap, prio, boost):
+    n = len(ops)
+    PLAN["args"] = (ops, deps, behind, succ, gap, prio)
+    prio = [p + boost.get(o["tag"], 0) for p, o in zip(prio, ops)]
+    left = [len(deps[j] | behind[j]) for j in range(n)]
+    ready = [0.0] * n
+    free = {q: 0.0 for q in "vstgyx"}
+    cand = {q: [] for q in free}
+    for j in range(n):
+        if left[j] == 0:
+            cand[ops[j]["q"]].append(j)
+    order = []
+    while len(order) < n:
+        best = None
+        for q in free:
+            if not cand[q]:
+                continue
+            t0 = max(free[q], min(ready[j] for j in cand[q]))
+            pick = max([j for j in cand[q] if ready[j] <= t0], key=lambda j: (prio[j], -j))
+            for j in cand[q]:
+                if ready[j] > t0 and prio[j] > prio[pick] and ready[j] - t0 < min(
+                        0.5 * ops[pick]["cost"], prio[j] - prio[pick]):
+                    pick = j
+            t1 = max(t0, ready[pick])
+            if best is None or t1 < best[0]:
+                best = (t1, pick)
+        t1, j = best
+        q = ops[j]["q"]
+        cand[q].remove(j)
+        order.append(j)
+        ops[j]["t"] = t1
+        end = t1 + ops[j]["cost"]
+        free[q] = end
+        for k in succ[j]:
+            ready[k] = max(ready[k], end + gap(j, k))
+            left[k] -= 1
+            if left[k] == 0:
+                cand[ops[k]["q"]].append(k)
+    return order
+
+
+def rank_program(g, core, T, topo):
+    rank = T.rank_of(core)
+    if rank is None:
+        return
+    ops = []
+    build(T, ops)
+    if "p" not in PLAN:
+        PLAN["p"] = plan(ops) + ([o["t"] for o in ops],)
+    order, deps, when = PLAN["p"]
+    eng = {"v": g.vector, "s": g.scalar, "t": g.tensor, "g": g, "y": g.sync}
+
+    def ring_mask(src):
+        m = -1
+        for c in T.cores:
+            if c != src:
+                m &= topo.mask(src, c)
+        return m
+
+    def width(m):
+        return bin(m).count("1")
+
+    pos, cnt, clock, snap, waits, marked = {}, {}, {q: {} for q in eng}, {}, {}, set()
+    first, final = {}, {}
+    for j in order:
+        o = ops[j]
+        q = o["q"]
+        if "grp" in o:
+            first.setdefault(o["grp"], j)
+            final[o["grp"]] = j
+        if q == "x":
+            pos[j], snap[j] = (("x", j), 1), {}
+            continue
+        need = {}
+        for i in deps[j]:
+            if q == "t" and ops[i]["q"] == "t":
+                continue
+            key, p = pos[i]
+            if clock[q].get(key, 0) < p and (key not in need or pos[need[key]][1] < p):
+                need[key] = i
+        waits[j] = []
+        for i in sorted(need.values(), key=lambda i: -when[i]):
+            key, p = pos[i]
+            if clock[q].get(key, 0) >= p:
+                continue
+            waits[j].append(i)
+            marked.add(i)
+            clock[q][key] = p
+            for kk, pp in snap[i].items():
+                if clock[q].get(kk, 0) < pp:
+                    clock[q][kk] = pp
+        snap[j] = dict(clock[q])
+        if o["kind"] == "c":
+            cnt[q] = cnt.get(q, 0) + 1
+            pos[j] = (q, cnt[q])
+        else:
+            pos[j] = ((o["kind"], j), 1)
+    sig, num, nd, sent, stores = {}, {}, 0, 0, []
+    for j in order:
+        o = ops[j]
+        q = o["q"]
+        if q == "x":
+            src = T.cores[(rank - o["hop"]) % N]
+            sig[j] = (T.sem[o["sem"]], width(ring_mask(src)))
+            continue
+        e = eng[q]
+        for i in waits[j]:
+            e.wait_ge(sig[i][0], sig[i][1])
+        if o["kind"] == "r":
+            dst = T.cores[(rank + o["hop"]) % N]
+            rid, pid = topo.addr(dst, core)
+            m = ring_mask(core)
+            g.remote_dma(o["dst"], o["src"], T.sem[o["sem"]], T.sem.sent, pid, rid, m)
+            sent += width(m)
+        elif o["kind"] == "d":
+            sig[j] = (T.sem["d%d" % nd], 16)
+            nd += 1
+            o["fn"](e, None).then_inc(sig[j][0], 16)
+            if j not in marked:
+                stores.append(j)
+        else:
+            ins = o["fn"](e, (first[o["grp"]] == j, final[o["grp"]] == j) if "grp" in o else None)
+            if j in marked:
+                num[q] = num.get(q, 0) + 1
+                sig[j] = (T.sem["q" + q], num[q])
+                ins.then_inc(sig[j][0], 1)
+    g.wait_ge(T.sem.sent, sent)
+    for j in stores:
+        g.sync.wait_ge(sig[j][0], sig[j][1])

@@ -1,51 +1,69 @@
+import math
+
 from concourse.mybir import AluOpType, AxisListType, ActivationFunctionType
 
 ALU = AluOpType
 ACT = ActivationFunctionType
 C, D, S, N = 1536, 256, 4, 4
 CH = 32
-PATH = ("ssvvvvvs", "ssvvvvhs")
-VRUNS = ((64, 128, "g"), (128, 192, "g"))
-CUT = ((), ())
+PATH = ("sssvvvss", "ssvvvvss")
+FIRST = "ssvvvvvs"
+PIECES = 4
+VRUNS = ((1, 64, 192, "v"), (4, 64, 128, "g"), (4, 128, 192, "g"))
+CUT = ((), (3, 7))
 POST = ((0, 8), (8, 16))
-VSUB = 32
-BOOST = {'vV1': 3000, 'vV2': 3000, 'sVC1': 4000, 'sVCT1': 4000, 'gJX1': 1500, 'vCA1': -1000, 'vCO2': -4000,
-         'vSC2': -200, 'gVQ7': 200, 'sG6': 500, 'vMK1': 4000, 'gPI1': 500, 'vPC1': -4000, 'vKKI1': -3500}
+ORDER = {
+    "v": "SC1 XM1 Ms5 K1I1 AIL1 A1 CO1 COH1 Mo3 SC2 XM2 Mo2 K1I2 AIL2 A2 CO2 Mo5 SC3 COH2 XM3 Mo4 KI1 FN1 NH1 KKI1 SC4 "
+         "XM4 KI2 KI3 FN2 PP1 PP2 HKO1 NH2 BB1 CA1+ CS1 D1 OHR1 X1 X2 X3 X4 LSC1 OH1 L1 X5 LSC2 LSC3 Ms3+ L2 DF1 DF2 DF3 "
+         "E1 DF4 CAH1+ DA1 MN2 MN1 OFF2 OFF1 DO1 A3 V1 KT1 YN1 A4 V2 O1 YN2 CA2+ KT2 Ms2+ MF1+ CAH2+ Ms6+ VQ2+ O2 VQ4+ "
+         "VQ1+ VQ3+ Ms4+",
+    "s": "Gs6 VCT1 Gs7 Ms6 Ms7 VCT2 Go0 Go1 Mo0 Mo1 Go6 Go7 Mo6 Mo7 RK1 Gs0+ Gs1+ DF1 DF3 DF2 Gs2+ YAB1 DF4 BV1 BX1 BA1 "
+         "DV1 BW1 Ms0+ Ms1+ VC1+ Ms2+ GF1+",
+}
+ROUNDS, SEED = 60000, 1
 PLAN = {}
 MAG = 12582912.0
 BIG = 8192.0
+KW = 8 * 17
+SP = 64
+STAY = 11.5 * 65536
+HELD = 1 << 23
+INORDER = False
+HLAT = 2000.0
+SLOW = (2000.0, 1.3)
 GC, SCT, CYC, PEC = 1.56, 3.8, 1.0, 0.5
 LX, LQ = 100.0, 60.0
 
 F, B, I, U, H = "float32", "bfloat16", "int32", "uint16", "float16"
 SB = {
-    "AO": (C, I), "AI": (C, I), "A": (C + 64, F), "O": (C + 64, F), "Y": (C, B), "V": (C + 64, B), "IOTA": (C, F),
+    "AO": (C, I), "AI": (C, I), "A": (C + 64, F), "O": (C + 64, F), "Y": (C, B), "V": (C + 64, B),
     "M0": (4096, B), "M1": (4096, B), "G0": (4096, B), "G1": (4096, B), "REP": (2048, B), "ONES": (512, B),
-    "Z0": (D, B), "VR": (4096, B), "VQ": (1024, B), "VCT": (D, B), "VC": (D, B),
-    "H16": (16, U), "CA16": (D, U), "CO16": (D, U), "CAF": (D + 16, F), "COF": (D + 16, F), "AF": (D + 16, F),
-    "FR": (D + 16, F), "OH": (D + 16, F), "SC0": (128, F), "SC1": (128, F), "XM0": (128, F), "XM1": (128, F),
-    "K1I": (16, I), "K2I": (16, I), "AIL": (16, I), "KKI": (16, I), "FI": (16, I), "A16": (16, U), "K16": (16, U),
-    "F16": (16, U), "NV": (16, F), "DF": (16, F), "E1": (16, F), "P16": (16, U), "NH16": (16, U),
-    "PR": (D, B), "R": (D, B), "JK": (D, B), "JV": (D, B), "CN": (2, F), "D16": (2, U), "TH2": (2, F),
-    "OHS": (32, F), "X": (128, H), "BA": (64, F), "DA": (32, F), "BW": (64, F), "DO": (32, F),
-    "BV": (64, B), "DV": (64, B), "YAB": (64, B), "LSC": (128, F), "L": (8, F), "L16": (8, U), "E": (8, F),
-    "DF0": (256, F), "DF1": (256, F), "MN": (2, F), "OK": (2, F), "OFF": (8, U),
-    "PI": (2, I), "PJ": (2, I), "PC": (8, F), "JN": (128, F), "JX": (128, F), "JG": (128, F), "JS": (128, F),
-    "IDB": (128, B), "NID": (128, B), "IDF": (128, F), "MASK": (128, F), "BLK": (128, H), "UD": (8, F), "WP": (8, B),
-    "WN": (8, B), "WH": (8, B), "KROW": (128, B), "NEG": (128, F), "CT": (128, F), "CT2": (128, F), "MK0": (128, B),
-    "MK1": (128, B), "OFS": (8, F), "DUM": (8, F), "CLI": (8, I), "CL": (8, U), "OHT": (16, F), "THR": (16, F),
-    "J8": (8, F), "J4": (8, F), "CB": (2, F),
+    "VR": (4096, B), "VQ": (1024, B), "VCT": (D, B), "VC": (D, B), "HI": (16, I),
+    "CA16": (D, U), "CO16": (D, U), "CAH": (D, H), "COH": (D, H), "KT": (C + 64, F), "YN": (C + 64, B),
+    "MF": (D, B), "GF": (D, F), "BX": (64, F), "KILL": (KW, F),
+    "SC0": (KW, F), "SC1": (KW, F), "XM0": (128, F), "XM1": (128, F),
+    "K1I": (16, I), "KI": (32, I), "FN": (40, I), "AIL": (24, I), "KKI": (24, I), "A16": (16, U),
+    "HKO": (64, F), "HT": (128, F), "PP": (32, B), "RK": (24, F), "BB": (32, B), "CS": (32, B), "D16": (2, U),
+    "OHR": (32, F), "OH": (32, F), "X": (160, H), "BA": (64, F), "DA": (32, F), "BW": (64, F), "DO": (32, F),
+    "BV": (64, B), "DV": (64, B), "YAB": (64, B), "LSC": (128, F), "L16": (8, U), "E": (8, F),
+    "DF0": (256, B), "DF1": (256, B), "MN0": (128, B), "MN1": (128, B), "OFF": (8, U),
+    "PI": (2, I), "PJ": (2, I), "PC": (8, F), "JX": (128, F), "JG": (128, F), "JS": (64, F),
+    "IDB": (128, B), "NID": (128, B), "IDH": (KW, B), "IDF": (128, F), "ZQ": (1024, B), "MASK": (128, F),
+    "BLK": (128, B), "NBK": (128, B), "BK2": (128, B), "TRI": (128, B), "UD": (8, F), "WP": (8, B),
+    "WN": (8, B), "WD": (8, B), "KROW": (KW, B), "NEG": (KW, F), "CT": (64, F), "CT2": (64, F), "MK0": (64, B),
+    "MK1": (64, B), "MKF": (64, F), "DUB": (8, B), "DUP": (8, F), "CLI": (16, I), "CL": (16, U),
+    "J4": (8, F), "TH2": (32, F), "RST": (32, B), "ODD": (32, F),
 }
 for _t in range(S):
-    SB["HI%d" % _t] = (16, I)
-    SB["NH%d" % _t] = (16, I)
-    SB["ZR%d" % _t] = (4096 + D, B)
-    SB["HR%d" % _t] = (D, F)
+    SB["H%d" % _t] = (16, U)
+    SB["HK%d" % _t] = (16, F)
+    SB["NH%d" % _t] = (16, U)
+    SB["ZR%d" % _t] = (4096 + 2 * D, B)
 SCRATCH = {k: ("sbuf", [128, v[0]], v[1]) for k, v in SB.items()}
 for _b in range(8):
     SCRATCH["P%d" % _b] = ("psum", [128, 512], F)
-SEMAPHORES = (["qv", "qs", "qt", "qg", "sent"] + ["d%d" % i for i in range(16)]
-              + ["za%d" % i for i in range(1, S)] + ["ha%d" % i for i in range(1, S)])
+SEMAPHORES = (["qv", "qs", "qt", "qg", "sent"] + ["d%d" % i for i in range(24)]
+              + [n + str(i) for n in ("za", "ha", "hb", "ka") for i in range(1, S)])
 
 
 def bits(lo, hi, st):
@@ -59,6 +77,7 @@ def bits(lo, hi, st):
 
 def build(T, ops):
     tags = {}
+    step = [-1]
 
     def a(name, lo=0, hi=None, st=1, p0=0, p1=128):
         if hi is None:
@@ -88,8 +107,9 @@ def build(T, ops):
                 rd.append((x[4][1], x[4][2]))
         o = dict(q=q, fn=fn, rd=rd, wr=wr, cost=cost, lat=0.0, kind="c")
         nm = q + (outs[0][1] if outs else "").rstrip("0123456789")
-        tags[nm] = tags.get(nm, 0) + 1
-        o["tag"] = nm + str(tags[nm])
+        tags[nm, step[0]] = tags.get((nm, step[0]), 0) + 1
+        o["tag"] = nm + str(tags[nm, step[0]])
+        o["step"] = step[0]
         o.update(kw)
         ops.append(o)
         return len(ops) - 1
@@ -147,6 +167,10 @@ def build(T, ops):
         c = max(min(64, lt[3]), rh[3]) * (4 if SCRATCH[lt[1]][2] == F else 1) * PEC + 10
         add("t", lambda e, k: e.matmul(out[0], lt[0], rh[0], k[0], k[1]), [out], [lt, rh], c, grp=grp, lat=60.0)
 
+    def mm16(outs, lts, rh, grp):
+        fn = lambda e, k: [e.matmul(o[0], l[0], rh[0], False, False) for o, l in zip(outs, lts)][-1]
+        add("t", fn, outs, lts + [rh], 16 * (min(64, lts[0][3]) * PEC + 10), grp=grp, lat=60.0)
+
     def iota(out, pat, base, cm):
         if SCRATCH[out[1]][2] == I:
             fn = lambda e, k: e.iota(out[0], pat, base, cm)
@@ -154,10 +178,13 @@ def build(T, ops):
             fn = lambda e, k: e.iota(out[0], pat, base, cm, allow_small_or_imprecise_dtypes=True)
         add("g", fn, [out], [], 130 + 2 * out[3] * CYC)
 
+    def pick(out, in_, pat, op, fill, base, cm):
+        add("g", lambda e, k: e.affine_select(out[0], in_[0], pat, op, fill, base, cm), [out], [in_],
+            170 + 2 * out[3] * CYC)
+
     def copy_on(q, out, in_):
         if q == "g":
-            add("g", lambda e, k: e.affine_select(out[0], in_[0], [[0, out[3]]], ALU.is_ge, 0.0, 0, 0), [out], [in_],
-                170 + 2 * out[3] * CYC)
+            pick(out, in_, [[0, out[3]]], ALU.is_ge, 0.0, 0, 0)
         elif q == "s":
             act(out, in_, ACT.Copy)
         else:
@@ -171,253 +198,319 @@ def build(T, ops):
         add("x", None, [dst], [], 0.0, kind="x", lat=lat, after=[j], hop=hop, sem=sem)
         return j
 
-    vch = [c for c in range(8) if PATH[0][c] == "v"] or [0]
+    vch = [c for c in range(8) if "v" in (PATH[0][c], FIRST[c])]
     z0, z1 = CH * vch[0], CH * (vch[-1] + 1)
     zt = 16 * (z1 - z0)
+    zr = zt + D
 
-    def segs(s, h):
+    def path(t, s):
+        return FIRST if t == s == 0 else PATH[s]
+
+    def segs(t, s, h):
         r = []
         for c in range(4 * h, 4 * h + 4):
-            k = PATH[s][c] in "sw"
+            k = s == 0 and path(t, s)[c] == "s"
             if r and r[-1][2] == k and r[-1][0] % 64 == 0 and c not in CUT[s]:
                 r[-1][1] += CH
             else:
                 r.append([c * CH, (c + 1) * CH, k])
         return r
 
-    def turned(dst, lo, src, s, gid):
+    def turned(dst, lo, src, so, s, gid):
         for h in (0, 1):
             if s == 0 or PATH[s][4 * h:4 * h + 4] != "vvvv":
-                mm(a("P7", 128 * h, 128 * h + 128), a(src, 128 * h, 128 * h + 128), a("IDB"), (gid, h))
+                mm(a("P7", 128 * h, 128 * h + 128), a(src, so + 128 * h, so + 128 * h + 128), a("IDB"), (gid, h))
                 act(a(dst, lo + 128 * h, lo + 128 * h + 128), a("P7", 128 * h, 128 * h + 128), ACT.Copy)
 
-    hc = C // 2
-    j = dma("s", T.Z0[:], T.zc[:], [a("Z0")], [], 2300.0)
-    dma("s", T.HI0[:], T.hd[:], [a("HI0")], [], 2300.0, [j])
-    j = dma("y", T.AO[:, 0:hc], T.ao[:, 0:hc], [a("AO", 0, hc)], [], 4000.0)
-    j = dma("y", T.AO[:, hc:C], T.ao[:, hc:C], [a("AO", hc, C)], [], 6000.0, [j])
+    hc = C // PIECES
+    j = dma("s", T.ZR0[:, zr:zr + D], T.zc[:], [a("ZR0", zr, zr + D)], [], 2300.0)
+    dma("s", T.HI[:], T.hd[:], [a("HI")], [], 2300.0, [j])
+    j = None
+    for lo in range(0, C, hc):
+        j = dma("y", T.AO[:, lo:lo + hc], T.ao[:, lo:lo + hc], [a("AO", lo, lo + hc)], [], 2000.0 + 4000.0 * (lo + hc) / C,
+                [j] if lo else [])
     j = dma("y", T.Y[:], T.yd[:], [a("Y")], [], 8000.0, [j])
-    dma("y", T.V[:, 0:C], T.ve[:], [a("V", 0, C)], [], 10000.0, [j])
+    j = dma("y", T.V[:, SP:SP + C], T.ve[:], [a("V", SP)], [], 10000.0, [j])
+    dma("y", T.YN[:, SP:SP + C], T.yd[:], [a("YN", SP)], [], 12000.0, [j])
 
     iota(a("PI", 0, 1), [[0, 1]], 0, 1)
-    iota(a("JN"), [[1, 128]], 0, 0)
     iota(a("JX"), [[0, 8], [1, 16]], 0, 0)
     iota(a("JG"), [[1, 8], [0, 16]], 0, 0)
-    iota(a("JS"), [[0, 4], [1, 32]], 0, 0)
-    iota(a("CLI"), [[16, 8]], 15, 0)
-    iota(a("J8"), [[0, 4], [int(BIG), 2]], 0, 0)
-    iota(a("J4"), [[0, 4], [16, 2]], C, 0)
+    iota(a("JS"), [[0, 2], [1, 32]], 0, 0)
+    iota(a("CLI"), [[-1, 2], [17, 8]], 16, 0)
+    iota(a("KROW"), [[0, 8], [-2048, 17]], 30720, 0)
+    iota(a("KROW", 16, KW, 17), [[0, 8]], -HELD, 0)
+    for lo in range(0, C + SP, 200):
+        iota(a("KT", lo, lo + 200), [[0, 200]], 0, 0)
+    iota(a("J4"), [[0, 4], [16, 2]], 0, 0)
+    iota(a("ODD"), [[2, 32]], 1, 0)
+    for nm, lo, n in (("FN", 32, 8), ("AIL", 16, 8), ("KKI", 16, 8), ("RK", 16, 8), ("A", 0, SP), ("O", 0, SP),
+                      ("V", 0, SP), ("YN", 0, SP)):
+        iota(a(nm, lo, lo + n), [[0, n]], 0, 0)
+    mset(a("ONES"), 1.0)
     ts(a("PJ", 0, 1), a("PI", 0, 1), 15, ALU.bitwise_and)
     ts(a("PJ", 1, 2), a("PI", 0, 1), 4, ALU.logical_shift_right)
-    pp, p16, pg, p17, ph, p32, q15, pf = (a("PC", j, j + 1) for j in range(8))
-    cp(pp, a("PI", 0, 1))
-    cp(a("PC", 1, 3), a("PJ"))
-    ts(p17, p16, 1.0, ALU.add)
-    ts(ph, p16, 0.5, ALU.add)
-    ts(p32, p16, 16.0, ALU.add)
-    ts(q15, p16, -1.0, ALU.mult, 15.0, ALU.add)
-    ts(pf, p16, 15.0, ALU.is_lt, 4096.0, ALU.mult)
-    mset(a("CB"), -511.0 / 512)
-    ts(a("IDB"), a("JN"), pp, ALU.is_equal)
-    ts(a("NID"), a("JN"), pp, ALU.is_equal, -1.0, ALU.mult)
-    ts(a("IDF"), a("JN"), pp, ALU.is_equal)
+    p16, pg, p32, q15, pf, kk, pd = (a("PC", j, j + 1) for j in range(7))
+    cp(a("PC", 0, 2), a("PJ"))
+    act(p32, p16, ACT.Identity, 16.0)
+    act(q15, p16, ACT.Identity, 15.0, -1.0)
+    act(kk, p16, ACT.Identity, HELD + 30720.0, -2048.0)
+    act(pd, p16, ACT.Sigmoid, 256 * 14.5, -256.0)
+    ops[-1]["cost"] += 1300.0
+    act(pf, pd, ACT.Identity, None, 4096.0)
+    act(pd, pf, ACT.Identity, -float(SP))
+    pick(a("IDB"), a("ONES", 0, 128), [[-1, 128]], ALU.is_equal, 0.0, 0, 1)
+    for nm, w in (("NID", -1.0), ("IDF", 1.0)):
+        act(a(nm), a("IDB"), ACT.Identity, None, w)
+    pick(a("IDH"), a("ONES", 0, KW), [[-16, 8], [-1, 17]], ALU.is_equal, 0.0, 0, 1)
+    iota(a("IDH", 16, KW, 17), [[0, 8]], 0, 0)
+    act(a("KILL"), a("IDH"), ACT.Identity, None, -1.0)
     ts(a("MASK"), a("JX"), p16, ALU.is_equal)
     ts(a("BLK"), a("JG"), pg, ALU.is_equal)
-    ts(a("UD"), a("JN", 0, 8), pg, ALU.is_equal)
-    for nm, w in (("WP", 32768.0), ("WN", -32768.0), ("WH", 16384.0)):
-        ts(a(nm), a("JN", 0, 8), pg, ALU.is_equal, w, ALU.mult)
-    ts(a("KROW"), a("JX"), -2048.0, ALU.mult, 30720.0, ALU.add)
-    ts(a("NEG"), a("JX"), 0.0, ALU.is_equal, -1.0e9, ALU.mult)
-    ts(a("CT"), a("JX"), p16, ALU.is_equal, -1.0e6, ALU.mult)
-    ts(a("CT2"), a("JX"), p17, ALU.is_equal, 4096.0, ALU.mult)
-    tt(a("CT"), a("CT"), a("CT2"), ALU.add)
-    ts(a("MK0"), a("JS"), p16, ALU.is_ge, BIG, ALU.mult)
-    ts(a("MK1"), a("JS"), p32, ALU.is_ge, BIG, ALU.mult)
-    ts(a("OFS"), a("J8"), pf, ALU.add)
-    ts(a("DUM"), a("J4"), p16, ALU.add)
+    for nm, w in (("NBK", -1.0), ("BK2", 2.0), ("TRI", -2.0)):
+        act(a(nm), a("BLK"), ACT.Identity, None, w)
+    pick(a("TRI"), a("TRI"), [[-1, 128]], ALU.is_gt, 0.0, 0, 1)
+    pick(a("TRI"), a("TRI"), [[-1, 128]], ALU.not_equal, -1.0, 0, 1)
+    for o, w in ((a("UD"), 1.0), (a("KILL", 16, KW, 17), 1.0), (a("WP"), 32768.0), (a("WN"), -32768.0),
+                 (a("WD"), 65536.0)):
+        act(o, a("BLK", 0, 128, 16), ACT.Identity, None, w)
+    mset(a("NEG"), 0.0)
+    mset(a("NEG", 0, KW, 17), -1.0e9)
+    act(a("CT"), a("MASK", 0, 64), ACT.Identity, None, -1.0e6)
+    act(a("CT2"), a("MASK", 0, 64), ACT.Identity, None, 4096.0)
+    tt(a("CT", 1, 64), a("CT", 1, 64), a("CT2", 0, 63), ALU.add)
+    for nm, p in (("MK0", p16), ("MK1", p32)):
+        ts(a("MKF"), a("JS"), p, ALU.is_ge, BIG, ALU.mult)
+        act(a(nm), a("MKF"), ACT.Identity, pf)
+    act(a("DUB"), a("J4"), ACT.Identity, p16)
+    act(a("DUP"), a("DUB"), ACT.Identity, pd)
+    act(a("TH2"), a("JG", 0, 32), ACT.Identity, p16, 16.0)
+    pick(a("RST"), a("ONES", 0, 32), [[0, 2], [1, 16]], ALU.not_equal, 0.0, 0, 0)
     cp(a("CL"), a("CLI"))
-    ts(a("OHT"), a("JN", 0, 16), q15, ALU.is_equal)
-    c0 = 0
-    for c in range(1, 9):
-        if c == 8 or (PATH[1][c] in "sw") != (PATH[1][c0] in "sw"):
-            mset(a("THR", 2 * c0, 2 * c), (4.0 if PATH[1][c0] in "sw" else 12.0) * 32768.0)
-            c0 = c
-    for nm in ("CAF", "COF", "AF", "FR", "OH"):
-        mset(a(nm, D, D + 16), 0.0)
-    for nm in ("A", "O", "V"):
-        mset(a(nm, C, C + 64), 0.0)
-    mset(a("ONES"), 1.0)
     for j in range(4):
         if any(PATH[s][c] != "v" for s in (0, 1) for c in (j, j + 4)):
-            o, i = a("REP", 512 * j, 512 * j + 512), a("ONES")
-            add("g", lambda e, k, o=o, i=i, j=j: e.affine_select(o[0], i[0], [[-1, CH], [0, 16]], ALU.is_equal, 0.0,
-                                                                 -CH * j, 1), [o], [i], 170 + 1024 * CYC)
-    for j in range(3):
-        iota(a("IOTA", 512 * j, 512 * j + 512), [[1, 512]], 512 * j, 0)
+            pick(a("REP", 512 * j, 512 * j + 512), a("ONES"), [[-1, CH], [0, 16]], ALU.is_equal, 0.0, -CH * j, 1)
+    cp(a("H0"), a("HI"))
+    ts(a("HK0"), a("HI"), STAY, ALU.add)
 
-    for lo in (0, hc):
+    for lo in range(0, C, hc):
         ts(a("AI", lo, lo + hc), a("AO", lo, lo + hc), 4095, ALU.bitwise_and)
-        cp(a("A", lo, lo + hc), a("AI", lo, lo + hc))
-        ts(a("O", lo, lo + hc), a("AO", lo, lo + hc), 1.0 / 4096, ALU.mult, MAG, ALU.add)
+        cp(a("A", SP + lo, SP + lo + hc), a("AI", lo, lo + hc))
+        ts(a("O", SP + lo, SP + lo + hc), a("AO", lo, lo + hc), 1.0 / 4096, ALU.mult, MAG, ALU.add)
 
     for k in range(16):
-        act(a("ZR0", k, zt, 16), a("Z0", z0, z1), ACT.Copy)
-    turned("ZR0", zt, "Z0", 0, "z0")
+        act(a("ZR0", k, zt, 16), a("ZR0", zr + z0, zr + z1), ACT.Copy)
+    turned("ZR0", zt, "ZR0", zr, 0, "z0")
 
-    def send_costs(t, after):
-        remote(a("ZR0", 0, zt + D), a("ZR%d" % t, 0, zt + D), t, "za%d" % t, 14000.0, after)
+    j = []
+    for t in range(1, S):
+        j = [remote(a("ZR0", zt, zr + D), a("ZR%d" % t, zt, zr + D), t, "za%d" % t, 5000.0, j)]
 
-    tabA, tabO, tabV, tabY = a("A", 0, C), a("O", 0, C), a("V", 0, C), a("Y")
+    def spread_costs(t):
+        d0, d1 = CH * PATH[0].index("v"), CH * (PATH[0].rindex("v") + 1)
+        for k in range(4):
+            copy_on("g", a("ZQ", 4 * d0 + k, 4 * d1, 4), a("ZR%d" % t, zr + d0, zr + d1))
+        for d in range(d0, d1, 48):
+            for k in range(4):
+                copy_on("g", a("ZR%d" % t, 16 * (d - z0) + k, 16 * (d + 48 - z0), 4), a("ZQ", 4 * d, 4 * (d + 48)))
+
+    tabA, tabO, tabV, tabY = a("A", SP), a("O", SP), a("V", SP), a("Y")
     nd = [0]
 
-    def stage(t, s, h):
-        M, G, offs, keyf = "M%d" % s, "G%d" % s, ("CA16", "CO16")[s], ("CAF", "COF")[s]
+    def early(t, s, h):
+        return t > 0 and s == h == 0
+
+    def judge(t, s, h):
+        M, G, offs, keyf = "M%d" % s, "G%d" % s, ("CA16", "CO16")[s], ("CAH", "COH")[s]
         tab = (tabY, tabV)[s]
         tr = a("VCT", 128 * h, 128 * h + 128) if s else a("ZR%d" % t, zt + 128 * h, zt + 128 * h + 128)
         bank, gid = "P%d" % (2 * s + h), ("k", t, s, h)
-        mm(a(bank, 0, 128), a(keyf, 128 * h, 128 * h + 128), a("IDF"), gid)
+        cp(a(keyf, 128 * h, 128 * h + 128), a(offs, 128 * h, 128 * h + 128))
+        mm(a(bank, 0, KW), a(keyf, 128 * h, 128 * h + 128), a("IDH"), gid)
+        if early(t, s, h):
+            mm(a(bank, 0, KW), a("ONES", 0, 128, 1, 0, 1), a("KROW", 0, KW, 1, 0, 1), gid)
         for c in range(4 * h, 4 * h + 4):
-            d, kind = c * CH, PATH[s][c]
-            if kind != "v":
-                g_, db, m = a(G, 16 * d, 16 * d + 512), a("P%d" % (4 + nd[0] % 2)), a(M, 16 * d, 16 * d + 512)
+            d, name = c * CH, "so"[s] + str(c)
+            m = a(M, 16 * d, 16 * d + 512)
+            if path(t, s)[c] == "s":
+                g_, db = a(G, 16 * d, 16 * d + 512), a("P%d" % (4 + nd[0] % 2))
                 nd[0] += 1
-                copy_on("v" if kind == "w" else "s", g_, ind(tab, a(offs, d, d + CH)))
+                act(g_, ind(tab, a(offs, d, d + CH)), ACT.Copy)
+                ops[-1]["tag"] = "sG" + name
                 mm(db, tr, a("REP", 512 * (c % 4), 512 * (c % 4) + 512), ("d", nd[0]))
-                if kind == "h":
-                    tt(m, db, g_, (ALU.min, ALU.is_lt)[s])
+                mm(db, a("NID"), g_, ("d", nd[0]))
+                if s == 0:
+                    act(m, db, ACT.Relu)
                 else:
-                    mm(db, a("NID"), g_, ("d", nd[0]))
-                    if s == 0:
-                        act(m, db, ACT.Relu)
-                    else:
-                        act(m, db, ACT.Sign, -0.5, -1.0)
+                    act(m, db, ACT.Sigmoid, -128.0, -256.0)
             else:
-                for d in range(d, d + CH, VSUB):
-                    rep = a("VR", 16 * d, 16 * (d + VSUB)) if s else a("ZR%d" % t, 16 * (d - z0), 16 * (d - z0 + VSUB))
-                    tt(a(M, 16 * d, 16 * (d + VSUB)), ind(tab, a(offs, d, d + VSUB)), rep, (ALU.min, ALU.is_gt)[s])
-        for d0, d1, sc in segs(s, h):
-            w = a(("WN", "WH")[s] if sc else "WP")
-            for k in range(16):
-                mm(a(bank, k, 128, 16, d0 - 128 * h, d1 - 128 * h), a(M, 16 * d0 + k, 16 * d1, 16), w, gid)
-        mm(a(bank, 0, 128), a("ONES", 0, 128, 1, 0, 1), a("KROW", 0, 128, 1, 0, 1), gid)
+                rep = a("VR", 16 * d, 16 * d + 512) if s else a("ZR%d" % t, 16 * (d - z0), 16 * (d - z0) + 512)
+                tt(m, ind(tab, a(offs, d, d + CH)), rep, (ALU.min, ALU.is_gt)[s])
+            ops[-1]["tag"] = ops[-1]["q"] + "M" + name
+        for d0, d1, sc in segs(t, s, h):
+            w = a("WD" if s else "WN" if sc else "WP")
+            mm16([a(bank, k, KW, 17, d0 - 128 * h, d1 - 128 * h) for k in range(16)],
+                 [a(M, 16 * d0 + k, 16 * d1, 16) for k in range(16)], w, gid)
+            if early(t, s, h) and sc:
+                mm(a(bank, 16, KW, 17, d0 - 128 * h, d1 - 128 * h), a("ZR%d" % t, zr + d0, zr + d1), w, gid)
+
+    def best(t, s, h):
+        bank, gid = "P%d" % (2 * s + h), ("k", t, s, h)
+        r = (128 * h, 128 * h + 128)
+        if early(t, s, h):
+            hl = a("H%d" % t, 8 * h, 8 * h + 8)
+            tt(a("MF", *r), ind(a("YN", SP), hl), a("ZR%d" % t, zr + r[0], zr + r[1]), ALU.min)
+            act(a("GF", *r), ind(a("KT", SP), hl), ACT.Copy)
+            mm(a(bank, 16, KW, 17), a("MF", *r), a("WP"), gid)
+            mm(a(bank, 0, KW), a("GF", *r), a("KILL"), gid)
+        else:
+            mm(a(bank, 0, KW), a("ONES", 0, 128, 1, 0, 1), a("KROW", 0, KW, 1, 0, 1), gid)
         sc_, xm = a("SC%d" % h), a("XM%d" % h)
-        scan(sc_, a("NEG"), a(bank, 0, 128), 0.0, ALU.add, ALU.max)
-        tt(xm, ind(sc_, a("CL")), a("MASK"), ALU.mult)
+        scan(sc_, a("NEG"), a(bank, 0, KW), 0.0, ALU.add, ALU.max)
+        tt(xm, ind(sc_, a("CL", 8 * s, 8 * s + 8)), a("MASK"), ALU.mult)
         lp = a("P6", 16 * s + 8 * h, 16 * s + 8 * h + 8)
         mm(lp, xm, a("UD"), ("l", t, s, h))
-        cp(a(("K1I", "K2I")[s], 8 * h, 8 * h + 8), lp)
+        return lp
 
+    def shares(t, h):
+        step[0] = t
+        cp(a("CA16", 128 * h, 128 * h + 128), ind(tabA, a("H%d" % t, 8 * h, 8 * h + 8)))
+        judge(t, 0, h)
+
+    shares(0, 0)
     for t in range(S):
         last = t == S - 1
-        tags.clear()
-        HI, NH = "HI%d" % t, "NH%d" % t
-        cp(a("H16"), a(HI))
-        for h in (0, 1):
-            cp(a("CA16", 128 * h, 128 * h + 128), ind(tabA, a("H16", 8 * h, 8 * h + 8)))
-        act(a("CAF", 0, D), ind(tabA, a("H16")), ACT.Copy)
-        act(a("VC"), ind(tabV, a("H16")), ACT.Copy)
-        turned("VCT", 0, "VC", 1, ("v", t))
-        for d0, d1, q in VRUNS:
+        shares(t, 1)
+        H16, NH = "H%d" % t, "NH%d" % t
+        act(a("VC"), ind(tabV, a(H16)), ACT.Copy)
+        turned("VCT", 0, "VC", 0, 1, ("v", t))
+        j0 = len(ops)
+        for w, d0, d1, q in VRUNS:
             for k in range(4):
-                copy_on(q, a("VQ", 4 * d0 + k, 4 * d1, 4), a("VC", d0, d1))
-            for k in range(4):
-                copy_on(q, a("VR", 16 * d0 + k, 16 * d1, 4), a("VQ", 4 * d0, 4 * d1))
-        if t == 0:
-            send_costs(1, [])
+                copy_on(q, a("VR" if w > 1 else "VQ", 4 * w * d0 + k, 4 * w * d1, 4),
+                        a("VQ" if w > 1 else "VC", w * d0, w * d1))
+        mine = [j for j in range(j0, len(ops)) if ops[j]["q"] == "g"]
+        for i, j in zip(mine, mine[1:]):
+            ops[j]["after"] = [i]
+        if not last:
+            spread_costs(t + 1)
         for h in (0, 1):
-            stage(t, 0, h)
             l = (8 * h, 8 * h + 8)
             r = (128 * h, 128 * h + 128)
+            cp(a("K1I", *l), best(t, 0, h))
             ts(a("AIL", *l), a("K1I", *l), 2047, ALU.bitwise_and)
             cp(a("A16", *l), a("AIL", *l))
             ts(a("CO16", *r), ind(tabO, a("A16", *l)), -MAG, ALU.add)
-            act(a("COF", *r), ind(tabO, a("A16", *l)), ACT.Identity, -MAG)
-        ts(a("KKI"), a("K1I"), 11, ALU.arith_shift_right, 15, ALU.bitwise_and)
-        cp(a("K16"), a("KKI"))
-        act(a("OH", 0, D), ind(a("OHT"), a("K16")), ACT.Copy)
+        ts(a("KKI", 0, 16), a("K1I"), 11, ALU.arith_shift_right, 15, ALU.bitwise_and)
+        nh, fi, hko = a("FN", 0, 16), a("FN", 16, 32), a("HKO", 16 * t, 16 * t + 16)
         for h in (0, 1):
-            stage(t, 1, h)
-        for l in POST:
-            r = (16 * l[0], 16 * l[1])
-            ts(a("FI", *l), a("K2I", *l), 2047, ALU.bitwise_and)
-            tt(a("NV", *l), a("K2I", *l), a("THR", *l), ALU.is_lt)
-            cp(a("F16", *l), a("FI", *l))
-            tt(a("DF", *l), a("FI", *l), a(HI, *l), ALU.subtract)
-            tt(a("E1", *l), a("DF", *l), a("NV", *l), ALU.mult)
-            ts(a("P16", *l), a("E1", *l), 0.0, ALU.not_equal)
-            tt(a(NH, *l), a("FI", *l), a("E1", *l), ALU.subtract)
-            act(a("AF", *r), ind(tabA, a("F16", *l)), ACT.Copy)
-            act(a("FR", *r), ind(a("IOTA"), a("F16", *l)), ACT.Copy)
-            cp(a("PR", *r), ind(a("JN"), a("P16", *l)))
-            scan(a("R", *r), a("PR", *r), a("PR", *r), a("R", 127, 128) if l[0] else 0.0, ALU.add, ALU.max)
+            l = (8 * h, 8 * h + 8)
+            judge(t, 1, h)
+            tt(a("KI", *l), best(t, 1, h), a("HK%d" % t, *l), ALU.max)
+            if h:
+                cp(a("KI", 16, 32), a("P6", 16, 32))
+            ts(a("FN", 8 * h, 8 + 24 * h), a("KI", 8 * h, 8 + 24 * h), 2047, ALU.bitwise_and)
+            if not last:
+                cp(a(NH, *l), a("FN", *l))
+                j = remote(a(NH, *l), a("H%d" % (t + 1), *l), 1, "h%s%d" % ("ab"[h], t + 1), HLAT)
+        pr, ps = a("PP", 0, 16), a("PP", 16, 32)
+        tt(pr, fi, nh, ALU.not_equal)
+        ts(hko, nh, STAY, ALU.add)
         if not last:
-            j = remote(a(NH), a("HI%d" % (t + 1)), 1, "ha%d" % (t + 1), 2500.0)
-            if t + 2 < S:
-                send_costs(t + 2, [j])
-        cp(a("NH16"), a(NH))
-        act(a("HR%d" % t), ind(a("IOTA"), a("NH16")), ACT.Copy)
-        dma("y", T.ho[:, t * D:(t + 1) * D], T["HR%d" % t][0:128:16, :], [], [a("HR%d" % t)], 2000.0)
-        act(a("JK"), a("R"), ACT.Sign, ph, -1.0, a("CN", 0, 1))
-        ts(a("JV"), a("R"), p32, ALU.is_le)
-        red(a("CN", 1, 2), a("JV"), ALU.add)
-        ts(a("D16", 0, 1), a("CN", 0, 1), 0.5, ALU.mult, 128.0, ALU.add)
-        cp(a("D16", 1, 2), a("CN", 1, 2))
-        ts(a("TH2"), a("CN"), 255.5, ALU.is_ge, 1.0e9, ALU.mult)
+            remote(hko, a("HK%d" % (t + 1)), 1, "ka%d" % (t + 1), HLAT, [j])
+            shares(t + 1, 0)
+            step[0] = t
+        else:
+            ht = a("P7", 0, 128, 1, 0, 64)
+            mm(ht, a("HKO"), a("IDF"), "ho")
+            act(a("HT", 0, 128, 1, 0, 64), ht, ACT.Identity, -STAY)
+            for c in range(8):
+                dma("y", T.ho[c:c + 1, :], T.HT[0:64, 16 * c:16 * c + 16], [], [a("HT")], 2000.0)
+        scan(ps, pr, pr, 0.0, ALU.add, ALU.max)
+        for u in (0, 1):
+            mm(a("P2", 16 * u, 16 * u + 16), a("BLK"), ps, ("c", t, u))
+        mm(a("P3", 0, 16), a("TRI"), pr, ("r", t))
+        mm(a("P3", 0, 16), a("BK2"), ps, ("r", t))
+        tt(a("BB"), a("P2", 0, 32), a("TH2"), ALU.is_gt)
+        act(a("RK", 0, 16), a("P3", 0, 16), ACT.Copy)
+        scan(a("CS"), a("RST"), a("BB"), 0.0, ALU.mult, ALU.subtract)
         d16 = a("D16")
-        cp(a("OHS"), ind(a("OH"), d16))
-        xs = [a("X", 32 * j, 32 * j + 32) for j in range(4)]
-        for j, nm in enumerate(("COF", "FR", "CAF", "AF")):
-            tt(xs[j], ind(a(nm), d16), a("OHS"), ALU.mult)
-        r0, r1 = a("P0", 0, 128), a("P1", 0, 128)
-        mm(r1, a("IDB"), a("MK1"), ("e", t, 1))
-        mm(r0, a("IDB"), a("MK0"), ("e", t, 0))
-        mm(r1, a("BLK"), a("X"), ("e", t, 1))
-        mm(r0, a("BLK"), a("X"), ("e", t, 0))
+        ts(d16, a("CS", 15, 32, 16), 16.0, ALU.add)
+        tt(a("OHR"), ind(a("RK"), d16), a("ODD"), ALU.is_equal)
+        xs = [a("X", 32 * j, 32 * j + 32) for j in range(5)]
+        for j, win in enumerate((a("KKI"), a("FN", 16, 40), a("FN", 0, 24), a("AIL"))):
+            tt(xs[j], ind(win, d16), a("OHR"), ALU.mult)
+        mm(a("P2", 0, 64), a("BLK"), a("X", 0, 64), ("e", t))
+        scan(a("LSC", 0, 32), a("CT", 0, 32), a("P2", 32, 64), 0.0, ALU.add, ALU.max)
+        ts(a("OH"), a("P2", 0, 32), q15, ALU.is_equal)
+        ts(a("L16", 0, 2), a("LSC", 15, 32, 16), pf, ALU.subtract)
+        tt(xs[4], ind(tabA, a("L16", 0, 2)), a("OH"), ALU.mult)
+        mm(a("P6", 32, 96), a("BLK"), a("X", 64, 128), ("a", t))
+        scan(a("LSC", 32, 96), a("CT", 0, 64), a("P6", 32, 96), 0.0, ALU.add, ALU.max)
+        mm(a("P7", 0, 32), a("BLK"), xs[4], ("b", t))
+        scan(a("LSC", 96, 128), a("CT", 0, 32), a("P7", 0, 32), 0.0, ALU.add, ALU.max)
+        ts(a("L16", 2, 8), a("LSC", 47, 128, 16), pf, ALU.subtract)
+        for w in (0, 1):
+            for u in (1, 0):
+                row = a(("P3", "P1")[w] if u else ("P6", "P2")[w], 256, 320)
+                mm(row, a("IDB"), a("MK%d" % u), ("x", t, w, u))
+                mm(row, a("BLK"), a("X", 32 + 64 * w, 96 + 64 * w), ("x", t, w, u))
+                for j in (0, 1):
+                    own = 64 * w + 32 * j + 16 * u + 15
+                    df = a("DF%d" % u, 128 * j + 64 * w, 128 * j + 64 * w + 64)
+                    if u:
+                        act(df, row, ACT.Abs, a("LSC", own, own + 1), -1.0)
+                    else:
+                        ts(df, row, a("LSC", own, own + 1), ALU.not_equal)
+        tt(a("E"), a("LSC", 15, 128, 16), a("DUP"), ALU.subtract)
+        for u in (0, 1):
+            scan(a("MN%d" % u), a("DF%d" % u, 0, 128), a("DF%d" % u, 128, 256), a("BB", 16 * u + 15, 16 * u + 16),
+                 ALU.min, ALU.min)
+            ts(a("OFF", u, 8, 2), a("E", u, 8, 2), a("MN%d" % u, 127, 128), ALU.mult, a("DUB", u, u + 1), ALU.add)
         if not last:
-            act(a("BA", 0, 32), ind(a("CAF"), d16), ACT.Copy)
-            act(a("BA", 32, 64), ind(a("AF"), d16), ACT.Copy)
-            tt(a("DA"), xs[3], xs[2], ALU.subtract)
-            tt(a("DO"), xs[1], xs[0], ALU.subtract)
-        scan(a("LSC"), a("CT"), r1, 0.0, ALU.add, ALU.max)
-        tt(a("L"), a("LSC", 15, 128, 16), a("OFS"), ALU.subtract)
-        for j in range(4):
-            lo = 64 * (j // 2)
-            ts(a("DF0", 64 * j, 64 * j + 64), a("P0", lo, lo + 64), a("L", 2 * j, 2 * j + 1), ALU.not_equal)
-            act(a("DF1", 64 * j, 64 * j + 64), a("P1", lo, lo + 64), ACT.Identity, a("L", 2 * j + 1, 2 * j + 2), -1.0)
-        cp(a("L16"), a("L"))
-        tt(a("E"), a("L"), a("DUM"), ALU.subtract)
-        act(a("JK"), a("DF0"), ACT.Identity, a("CB", 0, 1), 1.0, a("MN", 0, 1))
-        red(a("MN", 1, 2), a("DF1"), ALU.min, True)
-        tt(a("OK"), a("MN"), a("TH2"), ALU.is_gt)
-        for j in range(2):
-            ts(a("OFF", j, 8, 2), a("E", j, 8, 2), a("OK", j, j + 1), ALU.mult, a("DUM", j, j + 1), ALU.add)
+            act(a("BA"), ind(tabA, a("L16", 0, 4)), ACT.Copy)
+            act(a("BX"), ind(tabA, a("L16", 0, 4)), ACT.Identity, kk)
+            for bank, out, lo, hi in (("P6", "DO", 2, 1), ("P7", "DA", 3, 4)):
+                mm(a(bank, 128, 160), a("NBK"), xs[lo], (out, t))
+                mm(a(bank, 128, 160), a("BLK"), xs[hi], (out, t))
+                tt(a(out), a(bank, 128, 160), a("OH"), ALU.mult)
         act(a("YAB"), ind(tabY, a("L16", 4, 8)), ACT.Copy)
         act(a("BV"), ind(tabV, a("L16", 0, 4)), ACT.Copy)
-        tt(a("DV", 0, 32), a("YAB", 32, 64), a("YAB", 0, 32), ALU.subtract)
-        act(a("DV", 32, 64), a("DV", 0, 32), ACT.Identity, None, -1.0)
+        for j in (0, 1):
+            mm(a("P3", 32 * j, 32 * j + 32), a("IDB"), a("YAB", 32 * j, 32 * j + 32), ("v", t, j, 0))
+            mm(a("P3", 32 * j, 32 * j + 32), a("NID"), a("YAB", 32 - 32 * j, 64 - 32 * j), ("v", t, j, 0))
+        act(a("DV"), a("P3", 0, 64), ACT.Copy)
         if not last:
             act(a("BW"), ind(tabO, a("L16", 4, 8)), ACT.Copy)
-            for j, op in ((0, ALU.add), (1, ALU.subtract)):
+            for j in (0, 1):
+                o = a("OFF", 2 * j, 2 * j + 2)
+                tt(ind(a("KT"), o), a("BX", 32 - 32 * j, 64 - 32 * j), a("OH"), ALU.mult)
+                cp(ind(a("YN"), o), a("YAB", 32 * j, 32 * j + 32))
+            for j, op in ((0, ALU.subtract), (1, ALU.add)):
                 tt(ind(a("A"), a("OFF", 2 * j, 2 * j + 2)), a("BA", 32 * j, 32 * j + 32), a("DA"), op)
         for j in (0, 1):
             tt(ind(a("V"), a("OFF", 2 * j, 2 * j + 2)), a("BV", 32 * j, 32 * j + 32), a("DV", 32 * j, 32 * j + 32), ALU.add)
         if not last:
             for j, op in ((0, ALU.add), (1, ALU.subtract)):
                 tt(ind(a("O"), a("OFF", 4 + 2 * j, 6 + 2 * j)), a("BW", 32 * j, 32 * j + 32), a("DO"), op)
-    dma("y", T.vo[:], T.V[:, 0:C], [], [tabV], 4000.0)
+    dma("y", T.vo[:], T.V[:, SP:SP + C], [], [tabV], 4000.0)
 
 
 def plan(ops):
     n = len(ops)
     seen = {}
     deps = [set() for _ in range(n)]
+    later = [set() for _ in range(n)]
     for j, o in enumerate(ops):
         for wr, lst in ((False, o["rd"]), (True, o["wr"])):
             for name, m in lst:
                 psum = SCRATCH[name][0] == "psum"
                 for i, mi, wi in seen.get(name, ()):
                     if ((wi or wr) and mi & m) or (psum and ops[i]["q"] != o["q"]):
-                        deps[j].add(i)
+                        if INORDER and wr and ops[i]["q"] == o["q"] and ops[i]["kind"] == o["kind"] == "c":
+                            later[j].add(i)
+                        else:
+                            deps[j].add(i)
         for wr, lst in ((False, o["rd"]), (True, o["wr"])):
             for name, m in lst:
                 old = seen.get(name, [])
@@ -425,62 +518,169 @@ def plan(ops):
                     old = [x for x in old if x[1] & ~m]
                 seen[name] = old + [(j, m, wr)]
         deps[j].discard(j)
-    behind = [set(o.get("after", ())) for o in ops]
+    behind = [set(o.get("after", ())) | (x - {j}) for j, (o, x) in enumerate(zip(ops, later))]
+    held = {}
+    for j, o in enumerate(ops):
+        if "grp" in o:
+            grp, mine, before = held.get(o["wr"][0][0], (None, [], []))
+            if grp != o["grp"]:
+                grp, mine, before = o["grp"], [], mine
+            behind[j].update(before)
+            held[o["wr"][0][0]] = (grp, mine + [j], before)
     succ = [[] for _ in range(n)]
     for j in range(n):
         for i in deps[j] | behind[j]:
-            succ[i].append(j)
-
-    def gap(i, j):
-        if (ops[i]["q"] == "t" and ops[j]["q"] == "t") or i not in deps[j]:
-            return 0.0
-        return ops[i]["lat"] + (LQ if ops[i]["q"] == ops[j]["q"] else LX)
-
-    prio = [0.0] * n
-    for i in range(n - 1, -1, -1):
-        prio[i] = ops[i]["cost"] + max([gap(i, j) + prio[j] for j in succ[i]] + [ops[i]["lat"]])
-    return place(ops, deps, behind, succ, gap, prio, BOOST), deps
+            free = (ops[i]["q"] == "t" and ops[j]["q"] == "t") or i not in deps[j]
+            succ[i].append((j, 0.0 if free else ops[i]["lat"] + (LQ if ops[i]["q"] == ops[j]["q"] else LX)))
+    PLAN["args"] = (ops, succ)
+    order, start = refine(ops, succ, dispatch(ops, succ) if ORDER else [0.0] * n, ROUNDS)
+    for o, t in zip(ops, start):
+        o["t"] = t
+    return order, deps
 
 
-def place(ops, deps, behind, succ, gap, prio, boost):
+def dispatch(ops, succ):
     n = len(ops)
-    PLAN["args"] = (ops, deps, behind, succ, gap, prio)
-    prio = [p + boost.get(o["tag"], 0) for p, o in zip(prio, ops)]
-    left = [len(deps[j] | behind[j]) for j in range(n)]
-    ready = [0.0] * n
+    wish = [0.0] * n
+    for j in range(n - 1, -1, -1):
+        wish[j] = min([wish[m] - g for m, g in succ[j]] + [-ops[j]["lat"]]) - ops[j]["cost"]
+    where = {(o["tag"], o["step"]): j for j, o in enumerate(ops) if o["step"] >= 0}
+    succ = [list(s) for s in succ]
+    for q, text in ORDER.items():
+        row = [where.get((q + x.rstrip("+-"), t + x.count("+") - x.count("-"))) for t in range(-1, S + 1)
+               for x in text.split()]
+        row = [j for j in row if j is not None]
+        for i, j in zip(row, row[1:]):
+            succ[i].append((j, -ops[i]["cost"]))
+    left, ready, start = [0] * n, [0.0] * n, [0.0] * n
+    for s in succ:
+        for m, g in s:
+            left[m] += 1
     free = {q: 0.0 for q in "vstgyx"}
-    cand = {q: [] for q in free}
-    for j in range(n):
-        if left[j] == 0:
-            cand[ops[j]["q"]].append(j)
-    order = []
-    while len(order) < n:
+    cand = {q: [j for j in range(n) if not left[j] and ops[j]["q"] == q] for q in free}
+    for _ in range(n):
         best = None
-        for q in free:
-            if not cand[q]:
-                continue
-            t0 = max(free[q], min(ready[j] for j in cand[q]))
-            pick = max([j for j in cand[q] if ready[j] <= t0], key=lambda j: (prio[j], -j))
-            for j in cand[q]:
-                if ready[j] > t0 and prio[j] > prio[pick] and ready[j] - t0 < min(
-                        0.5 * ops[pick]["cost"], prio[j] - prio[pick]):
-                    pick = j
-            t1 = max(t0, ready[pick])
-            if best is None or t1 < best[0]:
-                best = (t1, pick)
-        t1, j = best
+        for q, c in cand.items():
+            if c:
+                t0 = max(free[q], min(ready[j] for j in c))
+                pick = min((j for j in c if ready[j] <= t0), key=lambda j: (wish[j], j))
+                for j in c:
+                    if wish[j] < wish[pick] and ready[j] - t0 < 0.5 * ops[pick]["cost"]:
+                        pick = j
+                if best is None or max(t0, ready[pick]) < best[0]:
+                    best = (max(t0, ready[pick]), pick)
+        t, j = best
+        cand[ops[j]["q"]].remove(j)
+        start[j] = t
+        free[ops[j]["q"]] = t = t + ops[j]["cost"]
+        for m, g in succ[j]:
+            ready[m] = max(ready[m], t + g)
+            left[m] -= 1
+            if not left[m]:
+                cand[ops[m]["q"]].append(m)
+    return start
+
+
+def refine(ops, succ, start, rounds, heat=80.0):
+    n = len(ops)
+    cost, lat = [o["cost"] for o in ops], [o["lat"] for o in ops]
+    slow = [SLOW[0] if o["q"] == "x" else o["cost"] * (SLOW[1] if o["q"] == "t" else 1) for o in ops]
+    tied = [set() for _ in range(n)]
+    for i in range(n):
+        for m, g in succ[i]:
+            tied[m].add(i)
+    up, dn, tail = [-1] * n, [-1] * n, {}
+    for j in sorted(range(n), key=lambda j: (start[j], j)):
         q = ops[j]["q"]
-        cand[q].remove(j)
-        order.append(j)
-        ops[j]["t"] = t1
-        end = t1 + ops[j]["cost"]
-        free[q] = end
-        for k in succ[j]:
-            ready[k] = max(ready[k], end + gap(j, k))
-            left[k] -= 1
-            if left[k] == 0:
-                cand[ops[k]["q"]].append(k)
-    return order
+        if q != "x":
+            if q in tail:
+                up[j], dn[tail[q]] = tail[q], j
+            tail[q] = j
+
+    def run():
+        left = [len(tied[j]) + (up[j] >= 0) for j in range(n)]
+        seq = [j for j in range(n) if not left[j]]
+        r, by, end, last = [0.0] * n, [-1] * n, 0.0, -1
+        r2, by2, end2, last2 = [0.0] * n, [-1] * n, 0.0, -1
+        for j in seq:
+            x, y = r[j] + cost[j], r2[j] + slow[j]
+            if x + lat[j] > end:
+                end, last = x + lat[j], j
+            if y + lat[j] > end2:
+                end2, last2 = y + lat[j], j
+            for m, g in succ[j]:
+                if x + g > r[m]:
+                    r[m], by[m] = x + g, j
+                if y + g > r2[m]:
+                    r2[m], by2[m] = y + g, j
+                left[m] -= 1
+                if not left[m]:
+                    seq.append(m)
+            m = dn[j]
+            if m >= 0:
+                if x > r[m]:
+                    r[m], by[m] = x, j
+                if y > r2[m]:
+                    r2[m], by2[m] = y, j
+                left[m] -= 1
+                if not left[m]:
+                    seq.append(m)
+        return ((end + end2) / 2, r, ((by, last), (by2, last2)), seq) if len(seq) == n else None
+
+    def move(w, p, s):
+        a, b = up[w], dn[w]
+        if a >= 0:
+            dn[a] = b
+        if b >= 0:
+            up[b] = a
+        p, s = (up[s] if p is None else p), (dn[p] if s is None else s)
+        up[w], dn[w] = p, s
+        if p >= 0:
+            dn[p] = w
+        if s >= 0:
+            up[s] = w
+        return a, b
+
+    seed = [SEED]
+
+    def draw(k):
+        seed[0] = (seed[0] * 1103515245 + 12345) % 2147483648
+        return (seed[0] >> 8) % k
+
+    best = cur = run()
+    arcs = None
+    for it in range(rounds):
+        if arcs is None:
+            arcs = []
+            for by, j in cur[2]:
+                while j >= 0:
+                    i = by[j]
+                    if i >= 0 and i == up[j] and i not in tied[j]:
+                        arcs.append((i, j))
+                    j = i
+        if not arcs:
+            break
+        u, v = arcs[draw(len(arcs))]
+        k = (0, 0, 1, 1, 2, 3, 5)[draw(7)]
+        if draw(2):
+            w, a = v, u
+            while k and up[a] >= 0 and up[a] not in tied[v]:
+                a, k = up[a], k - 1
+            old = move(w, None, a)
+        else:
+            w, a = u, v
+            while k and dn[a] >= 0 and u not in tied[dn[a]]:
+                a, k = dn[a], k - 1
+            old = move(w, a, None)
+        new = run()
+        if new and draw(1 << 20) < (1 << 20) * math.exp(min(0.0, (cur[0] - new[0]) / (heat * (1 - it / rounds) + 1))):
+            cur, arcs = new, None
+            if cur[0] < best[0]:
+                best = cur
+        else:
+            move(w, *old)
+    rank = {j: p for p, j in enumerate(best[3])}
+    return sorted(range(n), key=lambda j: (best[1][j], rank[j])), best[1]
 
 
 def rank_program(g, core, T, topo):

import math

from concourse.mybir import AluOpType, AxisListType, ActivationFunctionType

ALU = AluOpType
ACT = ActivationFunctionType
C, D, S, N = 1536, 256, 4, 4
CH = 32
PATH = ("sssvvvss", "ssvvvvss")
FIRST = "ssvvvvvs"
PIECES = 4
VRUNS = ((1, 64, 192, "v"), (4, 64, 128, "g"), (4, 128, 192, "g"))
CUT = ((), (3, 7))
POST = ((0, 8), (8, 16))
ORDER = {
    "v": "SC1 XM1 Ms5 K1I1 AIL1 A1 CO1 COH1 Mo3 SC2 XM2 Mo2 K1I2 AIL2 A2 CO2 Mo5 SC3 COH2 XM3 Mo4 KI1 FN1 NH1 KKI1 SC4 "
         "XM4 KI2 KI3 FN2 PP1 PP2 HKO1 NH2 BB1 CA1+ CS1 D1 OHR1 X1 X2 X3 X4 LSC1 OH1 L1 X5 LSC2 LSC3 Ms3+ L2 DF1 DF2 DF3 "
         "E1 DF4 CAH1+ DA1 MN2 MN1 OFF2 OFF1 DO1 A3 V1 KT1 YN1 A4 V2 O1 YN2 CA2+ KT2 Ms2+ MF1+ CAH2+ Ms6+ VQ2+ O2 VQ4+ "
         "VQ1+ VQ3+ Ms4+",
    "s": "Gs6 VCT1 Gs7 Ms6 Ms7 VCT2 Go0 Go1 Mo0 Mo1 Go6 Go7 Mo6 Mo7 RK1 Gs0+ Gs1+ DF1 DF3 DF2 Gs2+ YAB1 DF4 BV1 BX1 BA1 "
         "DV1 BW1 Ms0+ Ms1+ VC1+ Ms2+ GF1+",
}
ROUNDS, SEED = 60000, 1
PLAN = {}
MAG = 12582912.0
BIG = 8192.0
KW = 8 * 17
SP = 64
STAY = 11.5 * 65536
HELD = 1 << 23
INORDER = False
HLAT = 2000.0
SLOW = (2000.0, 1.3)
GC, SCT, CYC, PEC = 1.56, 3.8, 1.0, 0.5
LX, LQ = 100.0, 60.0

F, B, I, U, H = "float32", "bfloat16", "int32", "uint16", "float16"
SB = {
    "AO": (C, I), "AI": (C, I), "A": (C + 64, F), "O": (C + 64, F), "Y": (C, B), "V": (C + 64, B),
    "M0": (4096, B), "M1": (4096, B), "G0": (4096, B), "G1": (4096, B), "REP": (2048, B), "ONES": (512, B),
    "VR": (4096, B), "VQ": (1024, B), "VCT": (D, B), "VC": (D, B), "HI": (16, I),
    "CA16": (D, U), "CO16": (D, U), "CAH": (D, H), "COH": (D, H), "KT": (C + 64, F), "YN": (C + 64, B),
    "MF": (D, B), "GF": (D, F), "BX": (64, F), "KILL": (KW, F),
    "SC0": (KW, F), "SC1": (KW, F), "XM0": (128, F), "XM1": (128, F),
    "K1I": (16, I), "KI": (32, I), "FN": (40, I), "AIL": (24, I), "KKI": (24, I), "A16": (16, U),
    "HKO": (64, F), "HT": (128, F), "PP": (32, B), "RK": (24, F), "BB": (32, B), "CS": (32, B), "D16": (2, U),
    "OHR": (32, F), "OH": (32, F), "X": (160, H), "BA": (64, F), "DA": (32, F), "BW": (64, F), "DO": (32, F),
    "BV": (64, B), "DV": (64, B), "YAB": (64, B), "LSC": (128, F), "L16": (8, U), "E": (8, F),
    "DF0": (256, B), "DF1": (256, B), "MN0": (128, B), "MN1": (128, B), "OFF": (8, U),
    "PI": (2, I), "PJ": (2, I), "PC": (8, F), "JX": (128, F), "JG": (128, F), "JS": (64, F),
    "IDB": (128, B), "NID": (128, B), "IDH": (KW, B), "IDF": (128, F), "ZQ": (1024, B), "MASK": (128, F),
    "BLK": (128, B), "NBK": (128, B), "BK2": (128, B), "TRI": (128, B), "UD": (8, F), "WP": (8, B),
    "WN": (8, B), "WD": (8, B), "KROW": (KW, B), "NEG": (KW, F), "CT": (64, F), "CT2": (64, F), "MK0": (64, B),
    "MK1": (64, B), "MKF": (64, F), "DUB": (8, B), "DUP": (8, F), "CLI": (16, I), "CL": (16, U),
    "J4": (8, F), "TH2": (32, F), "RST": (32, B), "ODD": (32, F),
}
for _t in range(S):
    SB["H%d" % _t] = (16, U)
    SB["HK%d" % _t] = (16, F)
    SB["NH%d" % _t] = (16, U)
    SB["ZR%d" % _t] = (4096 + 2 * D, B)
SCRATCH = {k: ("sbuf", [128, v[0]], v[1]) for k, v in SB.items()}
for _b in range(8):
    SCRATCH["P%d" % _b] = ("psum", [128, 512], F)
SEMAPHORES = (["qv", "qs", "qt", "qg", "sent"] + ["d%d" % i for i in range(24)]
              + [n + str(i) for n in ("za", "ha", "hb", "ka") for i in range(1, S)])


def bits(lo, hi, st):
    if st == 1:
        return ((1 << (hi - lo)) - 1) << lo
    m = 0
    for c in range(lo, hi, st):
        m |= 1 << c
    return m


def build(T, ops):
    tags = {}
    step = [-1]

    def a(name, lo=0, hi=None, st=1, p0=0, p1=128):
        if hi is None:
            hi = SCRATCH[name][1][1]
        ap = T[name][p0:p1, lo:hi:st] if st != 1 else T[name][p0:p1, lo:hi]
        m = bits(lo, hi, st)
        if SCRATCH[name][0] == "psum":
            m = sum(m << (512 * k) for k in range(p0 // 32, (p1 + 31) // 32))
        return (ap, name, m, len(range(lo, hi, st)))

    def ind(win, off):
        return (win[0].indirect(off[0]), win[1], win[2], 16 * off[3], off)

    def two(*xs):
        return all(SCRATCH[x[1]][2] in (B, H, U) for x in xs)

    def add(q, fn, outs, ins, cost, **kw):
        rd, wr = [], []
        for x in ins:
            if isinstance(x, tuple):
                rd.append((x[1], x[2]))
                if len(x) == 5:
                    rd.append((x[4][1], x[4][2]))
        for x in outs:
            wr.append((x[1], x[2]))
            if len(x) == 5:
                rd.append((x[4][1], x[4][2]))
        o = dict(q=q, fn=fn, rd=rd, wr=wr, cost=cost, lat=0.0, kind="c")
        nm = q + (outs[0][1] if outs else "").rstrip("0123456789")
        tags[nm, step[0]] = tags.get((nm, step[0]), 0) + 1
        o["tag"] = nm + str(tags[nm, step[0]])
        o["step"] = step[0]
        o.update(kw)
        ops.append(o)
        return len(ops) - 1

    def v(x):
        return x[0] if isinstance(x, tuple) else x

    def vc(out, in0, per):
        if len(out) == 5:
            return 50 + out[3] * SCT * CYC
        if len(in0) == 5:
            return 50 + in0[3] * GC * CYC
        return 40 + max(64, out[3] * per) * CYC

    def cp(out, in_):
        add("v", lambda e, k: e.tensor_copy(out[0], in_[0]), [out], [in_], vc(out, in_, 0.5 if two(out, in_) else 1))

    def tt(out, in0, in1, op):
        per = 1 if SCRATCH[in0[1]][0] == "psum" else 2
        add("v", lambda e, k: e.tensor_tensor(out[0], in0[0], in1[0], op), [out], [in0, in1], vc(out, in0, per))

    def ts(out, in0, s1, op0, s2=None, op1=None):
        if op1 is None:
            fn = lambda e, k: e.tensor_scalar(out[0], in0[0], v(s1), None, op0)
        else:
            fn = lambda e, k: e.tensor_scalar(out[0], in0[0], v(s1), v(s2), op0, op1)
        add("v", fn, [out], [in0, s1, s2], vc(out, in0, 0.5 if two(out, in0) else 1))

    def scan(out, d0, d1, init, op0, op1):
        add("v", lambda e, k: e.tensor_tensor_scan(out[0], d0[0], d1[0], v(init), op0, op1), [out], [d0, d1, init],
            vc(out, d0, 0.5 if two(out, d0, d1) else 1))

    def red(out, in_, op, ab=False):
        if ab:
            fn = lambda e, k: e.tensor_reduce(out[0], in_[0], AxisListType.X, op, apply_absolute_value=True)
        else:
            fn = lambda e, k: e.tensor_reduce(out[0], in_[0], AxisListType.X, op)
        add("v", fn, [out], [in_], 40 + max(64, in_[3]) * CYC)

    def mset(out, c):
        add("v", lambda e, k: e.memset(out[0], c), [out], [], 40 + max(64, out[3] * (0.5 if two(out) else 1)) * CYC)

    def act(out, in_, func=ACT.Identity, bias=None, scale=1.0, acc=None):
        kw = {}
        if bias is not None:
            kw["bias"] = v(bias)
        if scale != 1.0:
            kw["scale"] = scale
        if acc is not None:
            kw["accum_out"] = acc[0]
        cost = 65 + in_[3] * GC * CYC if len(in_) == 5 else 80 + max(64, in_[3]) * CYC
        add("s", lambda e, k: e.activation(out[0], in_[0], func, **kw), [out] + ([acc] if acc else []), [in_, bias], cost)

    def mm(out, lt, rh, grp):
        c = max(min(64, lt[3]), rh[3]) * (4 if SCRATCH[lt[1]][2] == F else 1) * PEC + 10
        add("t", lambda e, k: e.matmul(out[0], lt[0], rh[0], k[0], k[1]), [out], [lt, rh], c, grp=grp, lat=60.0)

    def mm16(outs, lts, rh, grp):
        fn = lambda e, k: [e.matmul(o[0], l[0], rh[0], False, False) for o, l in zip(outs, lts)][-1]
        add("t", fn, outs, lts + [rh], 16 * (min(64, lts[0][3]) * PEC + 10), grp=grp, lat=60.0)

    def iota(out, pat, base, cm):
        if SCRATCH[out[1]][2] == I:
            fn = lambda e, k: e.iota(out[0], pat, base, cm)
        else:
            fn = lambda e, k: e.iota(out[0], pat, base, cm, allow_small_or_imprecise_dtypes=True)
        add("g", fn, [out], [], 130 + 2 * out[3] * CYC)

    def pick(out, in_, pat, op, fill, base, cm):
        add("g", lambda e, k: e.affine_select(out[0], in_[0], pat, op, fill, base, cm), [out], [in_],
            170 + 2 * out[3] * CYC)

    def copy_on(q, out, in_):
        if q == "g":
            pick(out, in_, [[0, out[3]]], ALU.is_ge, 0.0, 0, 0)
        elif q == "s":
            act(out, in_, ACT.Copy)
        else:
            cp(out, in_)

    def dma(q, out, in_, outs, ins, lat, after=()):
        return add(q, lambda e, k: e.dma_start(out, in_), outs, ins, 60.0, kind="d", lat=lat, after=list(after))

    def remote(src, dst, hop, sem, lat, after=()):
        j = add("g", None, [], [src], 300.0, kind="r", src=src[0], dst=dst[0], hop=hop, sem=sem, after=list(after))
        add("x", None, [dst], [], 0.0, kind="x", lat=lat, after=[j], hop=hop, sem=sem)
        return j

    vch = [c for c in range(8) if "v" in (PATH[0][c], FIRST[c])]
    z0, z1 = CH * vch[0], CH * (vch[-1] + 1)
    zt = 16 * (z1 - z0)
    zr = zt + D

    def path(t, s):
        return FIRST if t == s == 0 else PATH[s]

    def segs(t, s, h):
        r = []
        for c in range(4 * h, 4 * h + 4):
            k = s == 0 and path(t, s)[c] == "s"
            if r and r[-1][2] == k and r[-1][0] % 64 == 0 and c not in CUT[s]:
                r[-1][1] += CH
            else:
                r.append([c * CH, (c + 1) * CH, k])
        return r

    def turned(dst, lo, src, so, s, gid):
        for h in (0, 1):
            if s == 0 or PATH[s][4 * h:4 * h + 4] != "vvvv":
                mm(a("P7", 128 * h, 128 * h + 128), a(src, so + 128 * h, so + 128 * h + 128), a("IDB"), (gid, h))
                act(a(dst, lo + 128 * h, lo + 128 * h + 128), a("P7", 128 * h, 128 * h + 128), ACT.Copy)

    hc = C // PIECES
    j = dma("s", T.ZR0[:, zr:zr + D], T.zc[:], [a("ZR0", zr, zr + D)], [], 2300.0)
    dma("s", T.HI[:], T.hd[:], [a("HI")], [], 2300.0, [j])
    j = None
    for lo in range(0, C, hc):
        j = dma("y", T.AO[:, lo:lo + hc], T.ao[:, lo:lo + hc], [a("AO", lo, lo + hc)], [], 2000.0 + 4000.0 * (lo + hc) / C,
                [j] if lo else [])
    j = dma("y", T.Y[:], T.yd[:], [a("Y")], [], 8000.0, [j])
    j = dma("y", T.V[:, SP:SP + C], T.ve[:], [a("V", SP)], [], 10000.0, [j])
    dma("y", T.YN[:, SP:SP + C], T.yd[:], [a("YN", SP)], [], 12000.0, [j])

    iota(a("PI", 0, 1), [[0, 1]], 0, 1)
    iota(a("JX"), [[0, 8], [1, 16]], 0, 0)
    iota(a("JG"), [[1, 8], [0, 16]], 0, 0)
    iota(a("JS"), [[0, 2], [1, 32]], 0, 0)
    iota(a("CLI"), [[-1, 2], [17, 8]], 16, 0)
    iota(a("KROW"), [[0, 8], [-2048, 17]], 30720, 0)
    iota(a("KROW", 16, KW, 17), [[0, 8]], -HELD, 0)
    for lo in range(0, C + SP, 200):
        iota(a("KT", lo, lo + 200), [[0, 200]], 0, 0)
    iota(a("J4"), [[0, 4], [16, 2]], 0, 0)
    iota(a("ODD"), [[2, 32]], 1, 0)
    for nm, lo, n in (("FN", 32, 8), ("AIL", 16, 8), ("KKI", 16, 8), ("RK", 16, 8), ("A", 0, SP), ("O", 0, SP),
                      ("V", 0, SP), ("YN", 0, SP)):
        iota(a(nm, lo, lo + n), [[0, n]], 0, 0)
    mset(a("ONES"), 1.0)
    ts(a("PJ", 0, 1), a("PI", 0, 1), 15, ALU.bitwise_and)
    ts(a("PJ", 1, 2), a("PI", 0, 1), 4, ALU.logical_shift_right)
    p16, pg, p32, q15, pf, kk, pd = (a("PC", j, j + 1) for j in range(7))
    cp(a("PC", 0, 2), a("PJ"))
    act(p32, p16, ACT.Identity, 16.0)
    act(q15, p16, ACT.Identity, 15.0, -1.0)
    act(kk, p16, ACT.Identity, HELD + 30720.0, -2048.0)
    act(pd, p16, ACT.Sigmoid, 256 * 14.5, -256.0)
    ops[-1]["cost"] += 1300.0
    act(pf, pd, ACT.Identity, None, 4096.0)
    act(pd, pf, ACT.Identity, -float(SP))
    pick(a("IDB"), a("ONES", 0, 128), [[-1, 128]], ALU.is_equal, 0.0, 0, 1)
    for nm, w in (("NID", -1.0), ("IDF", 1.0)):
        act(a(nm), a("IDB"), ACT.Identity, None, w)
    pick(a("IDH"), a("ONES", 0, KW), [[-16, 8], [-1, 17]], ALU.is_equal, 0.0, 0, 1)
    iota(a("IDH", 16, KW, 17), [[0, 8]], 0, 0)
    act(a("KILL"), a("IDH"), ACT.Identity, None, -1.0)
    ts(a("MASK"), a("JX"), p16, ALU.is_equal)
    ts(a("BLK"), a("JG"), pg, ALU.is_equal)
    for nm, w in (("NBK", -1.0), ("BK2", 2.0), ("TRI", -2.0)):
        act(a(nm), a("BLK"), ACT.Identity, None, w)
    pick(a("TRI"), a("TRI"), [[-1, 128]], ALU.is_gt, 0.0, 0, 1)
    pick(a("TRI"), a("TRI"), [[-1, 128]], ALU.not_equal, -1.0, 0, 1)
    for o, w in ((a("UD"), 1.0), (a("KILL", 16, KW, 17), 1.0), (a("WP"), 32768.0), (a("WN"), -32768.0),
                 (a("WD"), 65536.0)):
        act(o, a("BLK", 0, 128, 16), ACT.Identity, None, w)
    mset(a("NEG"), 0.0)
    mset(a("NEG", 0, KW, 17), -1.0e9)
    act(a("CT"), a("MASK", 0, 64), ACT.Identity, None, -1.0e6)
    act(a("CT2"), a("MASK", 0, 64), ACT.Identity, None, 4096.0)
    tt(a("CT", 1, 64), a("CT", 1, 64), a("CT2", 0, 63), ALU.add)
    for nm, p in (("MK0", p16), ("MK1", p32)):
        ts(a("MKF"), a("JS"), p, ALU.is_ge, BIG, ALU.mult)
        act(a(nm), a("MKF"), ACT.Identity, pf)
    act(a("DUB"), a("J4"), ACT.Identity, p16)
    act(a("DUP"), a("DUB"), ACT.Identity, pd)
    act(a("TH2"), a("JG", 0, 32), ACT.Identity, p16, 16.0)
    pick(a("RST"), a("ONES", 0, 32), [[0, 2], [1, 16]], ALU.not_equal, 0.0, 0, 0)
    cp(a("CL"), a("CLI"))
    for j in range(4):
        if any(PATH[s][c] != "v" for s in (0, 1) for c in (j, j + 4)):
            pick(a("REP", 512 * j, 512 * j + 512), a("ONES"), [[-1, CH], [0, 16]], ALU.is_equal, 0.0, -CH * j, 1)
    cp(a("H0"), a("HI"))
    ts(a("HK0"), a("HI"), STAY, ALU.add)

    for lo in range(0, C, hc):
        ts(a("AI", lo, lo + hc), a("AO", lo, lo + hc), 4095, ALU.bitwise_and)
        cp(a("A", SP + lo, SP + lo + hc), a("AI", lo, lo + hc))
        ts(a("O", SP + lo, SP + lo + hc), a("AO", lo, lo + hc), 1.0 / 4096, ALU.mult, MAG, ALU.add)

    for k in range(16):
        act(a("ZR0", k, zt, 16), a("ZR0", zr + z0, zr + z1), ACT.Copy)
    turned("ZR0", zt, "ZR0", zr, 0, "z0")

    j = []
    for t in range(1, S):
        j = [remote(a("ZR0", zt, zr + D), a("ZR%d" % t, zt, zr + D), t, "za%d" % t, 5000.0, j)]

    def spread_costs(t):
        d0, d1 = CH * PATH[0].index("v"), CH * (PATH[0].rindex("v") + 1)
        for k in range(4):
            copy_on("g", a("ZQ", 4 * d0 + k, 4 * d1, 4), a("ZR%d" % t, zr + d0, zr + d1))
        for d in range(d0, d1, 48):
            for k in range(4):
                copy_on("g", a("ZR%d" % t, 16 * (d - z0) + k, 16 * (d + 48 - z0), 4), a("ZQ", 4 * d, 4 * (d + 48)))

    tabA, tabO, tabV, tabY = a("A", SP), a("O", SP), a("V", SP), a("Y")
    nd = [0]

    def early(t, s, h):
        return t > 0 and s == h == 0

    def judge(t, s, h):
        M, G, offs, keyf = "M%d" % s, "G%d" % s, ("CA16", "CO16")[s], ("CAH", "COH")[s]
        tab = (tabY, tabV)[s]
        tr = a("VCT", 128 * h, 128 * h + 128) if s else a("ZR%d" % t, zt + 128 * h, zt + 128 * h + 128)
        bank, gid = "P%d" % (2 * s + h), ("k", t, s, h)
        cp(a(keyf, 128 * h, 128 * h + 128), a(offs, 128 * h, 128 * h + 128))
        mm(a(bank, 0, KW), a(keyf, 128 * h, 128 * h + 128), a("IDH"), gid)
        if early(t, s, h):
            mm(a(bank, 0, KW), a("ONES", 0, 128, 1, 0, 1), a("KROW", 0, KW, 1, 0, 1), gid)
        for c in range(4 * h, 4 * h + 4):
            d, name = c * CH, "so"[s] + str(c)
            m = a(M, 16 * d, 16 * d + 512)
            if path(t, s)[c] == "s":
                g_, db = a(G, 16 * d, 16 * d + 512), a("P%d" % (4 + nd[0] % 2))
                nd[0] += 1
                act(g_, ind(tab, a(offs, d, d + CH)), ACT.Copy)
                ops[-1]["tag"] = "sG" + name
                mm(db, tr, a("REP", 512 * (c % 4), 512 * (c % 4) + 512), ("d", nd[0]))
                mm(db, a("NID"), g_, ("d", nd[0]))
                if s == 0:
                    act(m, db, ACT.Relu)
                else:
                    act(m, db, ACT.Sigmoid, -128.0, -256.0)
            else:
                rep = a("VR", 16 * d, 16 * d + 512) if s else a("ZR%d" % t, 16 * (d - z0), 16 * (d - z0) + 512)
                tt(m, ind(tab, a(offs, d, d + CH)), rep, (ALU.min, ALU.is_gt)[s])
            ops[-1]["tag"] = ops[-1]["q"] + "M" + name
        for d0, d1, sc in segs(t, s, h):
            w = a("WD" if s else "WN" if sc else "WP")
            mm16([a(bank, k, KW, 17, d0 - 128 * h, d1 - 128 * h) for k in range(16)],
                 [a(M, 16 * d0 + k, 16 * d1, 16) for k in range(16)], w, gid)
            if early(t, s, h) and sc:
                mm(a(bank, 16, KW, 17, d0 - 128 * h, d1 - 128 * h), a("ZR%d" % t, zr + d0, zr + d1), w, gid)

    def best(t, s, h):
        bank, gid = "P%d" % (2 * s + h), ("k", t, s, h)
        r = (128 * h, 128 * h + 128)
        if early(t, s, h):
            hl = a("H%d" % t, 8 * h, 8 * h + 8)
            tt(a("MF", *r), ind(a("YN", SP), hl), a("ZR%d" % t, zr + r[0], zr + r[1]), ALU.min)
            act(a("GF", *r), ind(a("KT", SP), hl), ACT.Copy)
            mm(a(bank, 16, KW, 17), a("MF", *r), a("WP"), gid)
            mm(a(bank, 0, KW), a("GF", *r), a("KILL"), gid)
        else:
            mm(a(bank, 0, KW), a("ONES", 0, 128, 1, 0, 1), a("KROW", 0, KW, 1, 0, 1), gid)
        sc_, xm = a("SC%d" % h), a("XM%d" % h)
        scan(sc_, a("NEG"), a(bank, 0, KW), 0.0, ALU.add, ALU.max)
        tt(xm, ind(sc_, a("CL", 8 * s, 8 * s + 8)), a("MASK"), ALU.mult)
        lp = a("P6", 16 * s + 8 * h, 16 * s + 8 * h + 8)
        mm(lp, xm, a("UD"), ("l", t, s, h))
        return lp

    def shares(t, h):
        step[0] = t
        cp(a("CA16", 128 * h, 128 * h + 128), ind(tabA, a("H%d" % t, 8 * h, 8 * h + 8)))
        judge(t, 0, h)

    shares(0, 0)
    for t in range(S):
        last = t == S - 1
        shares(t, 1)
        H16, NH = "H%d" % t, "NH%d" % t
        act(a("VC"), ind(tabV, a(H16)), ACT.Copy)
        turned("VCT", 0, "VC", 0, 1, ("v", t))
        j0 = len(ops)
        for w, d0, d1, q in VRUNS:
            for k in range(4):
                copy_on(q, a("VR" if w > 1 else "VQ", 4 * w * d0 + k, 4 * w * d1, 4),
                        a("VQ" if w > 1 else "VC", w * d0, w * d1))
        mine = [j for j in range(j0, len(ops)) if ops[j]["q"] == "g"]
        for i, j in zip(mine, mine[1:]):
            ops[j]["after"] = [i]
        if not last:
            spread_costs(t + 1)
        for h in (0, 1):
            l = (8 * h, 8 * h + 8)
            r = (128 * h, 128 * h + 128)
            cp(a("K1I", *l), best(t, 0, h))
            ts(a("AIL", *l), a("K1I", *l), 2047, ALU.bitwise_and)
            cp(a("A16", *l), a("AIL", *l))
            ts(a("CO16", *r), ind(tabO, a("A16", *l)), -MAG, ALU.add)
        ts(a("KKI", 0, 16), a("K1I"), 11, ALU.arith_shift_right, 15, ALU.bitwise_and)
        nh, fi, hko = a("FN", 0, 16), a("FN", 16, 32), a("HKO", 16 * t, 16 * t + 16)
        for h in (0, 1):
            l = (8 * h, 8 * h + 8)
            judge(t, 1, h)
            tt(a("KI", *l), best(t, 1, h), a("HK%d" % t, *l), ALU.max)
            if h:
                cp(a("KI", 16, 32), a("P6", 16, 32))
            ts(a("FN", 8 * h, 8 + 24 * h), a("KI", 8 * h, 8 + 24 * h), 2047, ALU.bitwise_and)
            if not last:
                cp(a(NH, *l), a("FN", *l))
                j = remote(a(NH, *l), a("H%d" % (t + 1), *l), 1, "h%s%d" % ("ab"[h], t + 1), HLAT)
        pr, ps = a("PP", 0, 16), a("PP", 16, 32)
        tt(pr, fi, nh, ALU.not_equal)
        ts(hko, nh, STAY, ALU.add)
        if not last:
            remote(hko, a("HK%d" % (t + 1)), 1, "ka%d" % (t + 1), HLAT, [j])
            shares(t + 1, 0)
            step[0] = t
        else:
            ht = a("P7", 0, 128, 1, 0, 64)
            mm(ht, a("HKO"), a("IDF"), "ho")
            act(a("HT", 0, 128, 1, 0, 64), ht, ACT.Identity, -STAY)
            for c in range(8):
                dma("y", T.ho[c:c + 1, :], T.HT[0:64, 16 * c:16 * c + 16], [], [a("HT")], 2000.0)
        scan(ps, pr, pr, 0.0, ALU.add, ALU.max)
        for u in (0, 1):
            mm(a("P2", 16 * u, 16 * u + 16), a("BLK"), ps, ("c", t, u))
        mm(a("P3", 0, 16), a("TRI"), pr, ("r", t))
        mm(a("P3", 0, 16), a("BK2"), ps, ("r", t))
        tt(a("BB"), a("P2", 0, 32), a("TH2"), ALU.is_gt)
        act(a("RK", 0, 16), a("P3", 0, 16), ACT.Copy)
        scan(a("CS"), a("RST"), a("BB"), 0.0, ALU.mult, ALU.subtract)
        d16 = a("D16")
        ts(d16, a("CS", 15, 32, 16), 16.0, ALU.add)
        tt(a("OHR"), ind(a("RK"), d16), a("ODD"), ALU.is_equal)
        xs = [a("X", 32 * j, 32 * j + 32) for j in range(5)]
        for j, win in enumerate((a("KKI"), a("FN", 16, 40), a("FN", 0, 24), a("AIL"))):
            tt(xs[j], ind(win, d16), a("OHR"), ALU.mult)
        mm(a("P2", 0, 64), a("BLK"), a("X", 0, 64), ("e", t))
        scan(a("LSC", 0, 32), a("CT", 0, 32), a("P2", 32, 64), 0.0, ALU.add, ALU.max)
        ts(a("OH"), a("P2", 0, 32), q15, ALU.is_equal)
        ts(a("L16", 0, 2), a("LSC", 15, 32, 16), pf, ALU.subtract)
        tt(xs[4], ind(tabA, a("L16", 0, 2)), a("OH"), ALU.mult)
        mm(a("P6", 32, 96), a("BLK"), a("X", 64, 128), ("a", t))
        scan(a("LSC", 32, 96), a("CT", 0, 64), a("P6", 32, 96), 0.0, ALU.add, ALU.max)
        mm(a("P7", 0, 32), a("BLK"), xs[4], ("b", t))
        scan(a("LSC", 96, 128), a("CT", 0, 32), a("P7", 0, 32), 0.0, ALU.add, ALU.max)
        ts(a("L16", 2, 8), a("LSC", 47, 128, 16), pf, ALU.subtract)
        for w in (0, 1):
            for u in (1, 0):
                row = a(("P3", "P1")[w] if u else ("P6", "P2")[w], 256, 320)
                mm(row, a("IDB"), a("MK%d" % u), ("x", t, w, u))
                mm(row, a("BLK"), a("X", 32 + 64 * w, 96 + 64 * w), ("x", t, w, u))
                for j in (0, 1):
                    own = 64 * w + 32 * j + 16 * u + 15
                    df = a("DF%d" % u, 128 * j + 64 * w, 128 * j + 64 * w + 64)
                    if u:
                        act(df, row, ACT.Abs, a("LSC", own, own + 1), -1.0)
                    else:
                        ts(df, row, a("LSC", own, own + 1), ALU.not_equal)
        tt(a("E"), a("LSC", 15, 128, 16), a("DUP"), ALU.subtract)
        for u in (0, 1):
            scan(a("MN%d" % u), a("DF%d" % u, 0, 128), a("DF%d" % u, 128, 256), a("BB", 16 * u + 15, 16 * u + 16),
                 ALU.min, ALU.min)
            ts(a("OFF", u, 8, 2), a("E", u, 8, 2), a("MN%d" % u, 127, 128), ALU.mult, a("DUB", u, u + 1), ALU.add)
        if not last:
            act(a("BA"), ind(tabA, a("L16", 0, 4)), ACT.Copy)
            act(a("BX"), ind(tabA, a("L16", 0, 4)), ACT.Identity, kk)
            for bank, out, lo, hi in (("P6", "DO", 2, 1), ("P7", "DA", 3, 4)):
                mm(a(bank, 128, 160), a("NBK"), xs[lo], (out, t))
                mm(a(bank, 128, 160), a("BLK"), xs[hi], (out, t))
                tt(a(out), a(bank, 128, 160), a("OH"), ALU.mult)
        act(a("YAB"), ind(tabY, a("L16", 4, 8)), ACT.Copy)
        act(a("BV"), ind(tabV, a("L16", 0, 4)), ACT.Copy)
        for j in (0, 1):
            mm(a("P3", 32 * j, 32 * j + 32), a("IDB"), a("YAB", 32 * j, 32 * j + 32), ("v", t, j, 0))
            mm(a("P3", 32 * j, 32 * j + 32), a("NID"), a("YAB", 32 - 32 * j, 64 - 32 * j), ("v", t, j, 0))
        act(a("DV"), a("P3", 0, 64), ACT.Copy)
        if not last:
            act(a("BW"), ind(tabO, a("L16", 4, 8)), ACT.Copy)
            for j in (0, 1):
                o = a("OFF", 2 * j, 2 * j + 2)
                tt(ind(a("KT"), o), a("BX", 32 - 32 * j, 64 - 32 * j), a("OH"), ALU.mult)
                cp(ind(a("YN"), o), a("YAB", 32 * j, 32 * j + 32))
            for j, op in ((0, ALU.subtract), (1, ALU.add)):
                tt(ind(a("A"), a("OFF", 2 * j, 2 * j + 2)), a("BA", 32 * j, 32 * j + 32), a("DA"), op)
        for j in (0, 1):
            tt(ind(a("V"), a("OFF", 2 * j, 2 * j + 2)), a("BV", 32 * j, 32 * j + 32), a("DV", 32 * j, 32 * j + 32), ALU.add)
        if not last:
            for j, op in ((0, ALU.add), (1, ALU.subtract)):
                tt(ind(a("O"), a("OFF", 4 + 2 * j, 6 + 2 * j)), a("BW", 32 * j, 32 * j + 32), a("DO"), op)
    dma("y", T.vo[:], T.V[:, SP:SP + C], [], [tabV], 4000.0)


def plan(ops):
    n = len(ops)
    seen = {}
    deps = [set() for _ in range(n)]
    later = [set() for _ in range(n)]
    for j, o in enumerate(ops):
        for wr, lst in ((False, o["rd"]), (True, o["wr"])):
            for name, m in lst:
                psum = SCRATCH[name][0] == "psum"
                for i, mi, wi in seen.get(name, ()):
                    if ((wi or wr) and mi & m) or (psum and ops[i]["q"] != o["q"]):
                        if INORDER and wr and ops[i]["q"] == o["q"] and ops[i]["kind"] == o["kind"] == "c":
                            later[j].add(i)
                        else:
                            deps[j].add(i)
        for wr, lst in ((False, o["rd"]), (True, o["wr"])):
            for name, m in lst:
                old = seen.get(name, [])
                if wr:
                    old = [x for x in old if x[1] & ~m]
                seen[name] = old + [(j, m, wr)]
        deps[j].discard(j)
    behind = [set(o.get("after", ())) | (x - {j}) for j, (o, x) in enumerate(zip(ops, later))]
    held = {}
    for j, o in enumerate(ops):
        if "grp" in o:
            grp, mine, before = held.get(o["wr"][0][0], (None, [], []))
            if grp != o["grp"]:
                grp, mine, before = o["grp"], [], mine
            behind[j].update(before)
            held[o["wr"][0][0]] = (grp, mine + [j], before)
    succ = [[] for _ in range(n)]
    for j in range(n):
        for i in deps[j] | behind[j]:
            free = (ops[i]["q"] == "t" and ops[j]["q"] == "t") or i not in deps[j]
            succ[i].append((j, 0.0 if free else ops[i]["lat"] + (LQ if ops[i]["q"] == ops[j]["q"] else LX)))
    PLAN["args"] = (ops, succ)
    order, start = refine(ops, succ, dispatch(ops, succ) if ORDER else [0.0] * n, ROUNDS)
    for o, t in zip(ops, start):
        o["t"] = t
    return order, deps


def dispatch(ops, succ):
    n = len(ops)
    wish = [0.0] * n
    for j in range(n - 1, -1, -1):
        wish[j] = min([wish[m] - g for m, g in succ[j]] + [-ops[j]["lat"]]) - ops[j]["cost"]
    where = {(o["tag"], o["step"]): j for j, o in enumerate(ops) if o["step"] >= 0}
    succ = [list(s) for s in succ]
    for q, text in ORDER.items():
        row = [where.get((q + x.rstrip("+-"), t + x.count("+") - x.count("-"))) for t in range(-1, S + 1)
               for x in text.split()]
        row = [j for j in row if j is not None]
        for i, j in zip(row, row[1:]):
            succ[i].append((j, -ops[i]["cost"]))
    left, ready, start = [0] * n, [0.0] * n, [0.0] * n
    for s in succ:
        for m, g in s:
            left[m] += 1
    free = {q: 0.0 for q in "vstgyx"}
    cand = {q: [j for j in range(n) if not left[j] and ops[j]["q"] == q] for q in free}
    for _ in range(n):
        best = None
        for q, c in cand.items():
            if c:
                t0 = max(free[q], min(ready[j] for j in c))
                pick = min((j for j in c if ready[j] <= t0), key=lambda j: (wish[j], j))
                for j in c:
                    if wish[j] < wish[pick] and ready[j] - t0 < 0.5 * ops[pick]["cost"]:
                        pick = j
                if best is None or max(t0, ready[pick]) < best[0]:
                    best = (max(t0, ready[pick]), pick)
        t, j = best
        cand[ops[j]["q"]].remove(j)
        start[j] = t
        free[ops[j]["q"]] = t = t + ops[j]["cost"]
        for m, g in succ[j]:
            ready[m] = max(ready[m], t + g)
            left[m] -= 1
            if not left[m]:
                cand[ops[m]["q"]].append(m)
    return start


def refine(ops, succ, start, rounds, heat=80.0):
    n = len(ops)
    cost, lat = [o["cost"] for o in ops], [o["lat"] for o in ops]
    slow = [SLOW[0] if o["q"] == "x" else o["cost"] * (SLOW[1] if o["q"] == "t" else 1) for o in ops]
    tied = [set() for _ in range(n)]
    for i in range(n):
        for m, g in succ[i]:
            tied[m].add(i)
    up, dn, tail = [-1] * n, [-1] * n, {}
    for j in sorted(range(n), key=lambda j: (start[j], j)):
        q = ops[j]["q"]
        if q != "x":
            if q in tail:
                up[j], dn[tail[q]] = tail[q], j
            tail[q] = j

    def run():
        left = [len(tied[j]) + (up[j] >= 0) for j in range(n)]
        seq = [j for j in range(n) if not left[j]]
        r, by, end, last = [0.0] * n, [-1] * n, 0.0, -1
        r2, by2, end2, last2 = [0.0] * n, [-1] * n, 0.0, -1
        for j in seq:
            x, y = r[j] + cost[j], r2[j] + slow[j]
            if x + lat[j] > end:
                end, last = x + lat[j], j
            if y + lat[j] > end2:
                end2, last2 = y + lat[j], j
            for m, g in succ[j]:
                if x + g > r[m]:
                    r[m], by[m] = x + g, j
                if y + g > r2[m]:
                    r2[m], by2[m] = y + g, j
                left[m] -= 1
                if not left[m]:
                    seq.append(m)
            m = dn[j]
            if m >= 0:
                if x > r[m]:
                    r[m], by[m] = x, j
                if y > r2[m]:
                    r2[m], by2[m] = y, j
                left[m] -= 1
                if not left[m]:
                    seq.append(m)
        return ((end + end2) / 2, r, ((by, last), (by2, last2)), seq) if len(seq) == n else None

    def move(w, p, s):
        a, b = up[w], dn[w]
        if a >= 0:
            dn[a] = b
        if b >= 0:
            up[b] = a
        p, s = (up[s] if p is None else p), (dn[p] if s is None else s)
        up[w], dn[w] = p, s
        if p >= 0:
            dn[p] = w
        if s >= 0:
            up[s] = w
        return a, b

    seed = [SEED]

    def draw(k):
        seed[0] = (seed[0] * 1103515245 + 12345) % 2147483648
        return (seed[0] >> 8) % k

    best = cur = run()
    arcs = None
    for it in range(rounds):
        if arcs is None:
            arcs = []
            for by, j in cur[2]:
                while j >= 0:
                    i = by[j]
                    if i >= 0 and i == up[j] and i not in tied[j]:
                        arcs.append((i, j))
                    j = i
        if not arcs:
            break
        u, v = arcs[draw(len(arcs))]
        k = (0, 0, 1, 1, 2, 3, 5)[draw(7)]
        if draw(2):
            w, a = v, u
            while k and up[a] >= 0 and up[a] not in tied[v]:
                a, k = up[a], k - 1
            old = move(w, None, a)
        else:
            w, a = u, v
            while k and dn[a] >= 0 and u not in tied[dn[a]]:
                a, k = dn[a], k - 1
            old = move(w, a, None)
        new = run()
        if new and draw(1 << 20) < (1 << 20) * math.exp(min(0.0, (cur[0] - new[0]) / (heat * (1 - it / rounds) + 1))):
            cur, arcs = new, None
            if cur[0] < best[0]:
                best = cur
        else:
            move(w, *old)
    rank = {j: p for p, j in enumerate(best[3])}
    return sorted(range(n), key=lambda j: (best[1][j], rank[j])), best[1]


def rank_program(g, core, T, topo):
    rank = T.rank_of(core)
    if rank is None:
        return
    ops = []
    build(T, ops)
    if "p" not in PLAN:
        PLAN["p"] = plan(ops) + ([o["t"] for o in ops],)
    order, deps, when = PLAN["p"]
    eng = {"v": g.vector, "s": g.scalar, "t": g.tensor, "g": g, "y": g.sync}

    def ring_mask(src):
        m = -1
        for c in T.cores:
            if c != src:
                m &= topo.mask(src, c)
        return m

    def width(m):
        return bin(m).count("1")

    pos, cnt, clock, snap, waits, marked = {}, {}, {q: {} for q in eng}, {}, {}, set()
    first, final = {}, {}
    for j in order:
        o = ops[j]
        q = o["q"]
        if "grp" in o:
            first.setdefault(o["grp"], j)
            final[o["grp"]] = j
        if q == "x":
            pos[j], snap[j] = (("x", j), 1), {}
            continue
        need = {}
        for i in deps[j]:
            if q == "t" and ops[i]["q"] == "t":
                continue
            key, p = pos[i]
            if clock[q].get(key, 0) < p and (key not in need or pos[need[key]][1] < p):
                need[key] = i
        waits[j] = []
        for i in sorted(need.values(), key=lambda i: -when[i]):
            key, p = pos[i]
            if clock[q].get(key, 0) >= p:
                continue
            waits[j].append(i)
            marked.add(i)
            clock[q][key] = p
            for kk, pp in snap[i].items():
                if clock[q].get(kk, 0) < pp:
                    clock[q][kk] = pp
        snap[j] = dict(clock[q])
        if o["kind"] == "c":
            cnt[q] = cnt.get(q, 0) + 1
            pos[j] = (q, cnt[q])
        else:
            pos[j] = ((o["kind"], j), 1)
    sig, num, nd, sent, stores = {}, {}, 0, 0, []
    for j in order:
        o = ops[j]
        q = o["q"]
        if q == "x":
            src = T.cores[(rank - o["hop"]) % N]
            sig[j] = (T.sem[o["sem"]], width(ring_mask(src)))
            continue
        e = eng[q]
        for i in waits[j]:
            e.wait_ge(sig[i][0], sig[i][1])
        if o["kind"] == "r":
            dst = T.cores[(rank + o["hop"]) % N]
            rid, pid = topo.addr(dst, core)
            m = ring_mask(core)
            g.remote_dma(o["dst"], o["src"], T.sem[o["sem"]], T.sem.sent, pid, rid, m)
            sent += width(m)
        elif o["kind"] == "d":
            sig[j] = (T.sem["d%d" % nd], 16)
            nd += 1
            o["fn"](e, None).then_inc(sig[j][0], 16)
            if j not in marked:
                stores.append(j)
        else:
            ins = o["fn"](e, (first[o["grp"]] == j, final[o["grp"]] == j) if "grp" in o else None)
            if j in marked:
                num[q] = num.get(q, 0) + 1
                sig[j] = (T.sem["q" + q], num[q])
                ins.then_inc(sig[j][0], 1)
    g.wait_ge(T.sem.sent, sent)
    for j in stores:
        g.sync.wait_ge(sig[j][0], sig[j][1])
